import numpy as np
import ml_dtypes


def mxq(x, axis, fmt="e4m3"):
    dtype, down = {"e4m3": (ml_dtypes.float8_e4m3fn, 7), "e5m2": (ml_dtypes.float8_e5m2, 14)}[fmt]
    v = np.moveaxis(np.asarray(x, np.float32).astype(ml_dtypes.bfloat16).astype(np.float64), axis, -1)
    blocks = v.reshape(v.shape[:-1] + (-1, 32))
    amax = np.abs(blocks).max(-1, keepdims=True)
    byte = np.maximum(np.where(amax > 0, np.frexp(amax)[1] - 1 + 127, 0) - down, 1)
    scale = np.exp2(byte - 127.0)
    codes = (blocks / scale).astype(np.float32).astype(dtype).astype(np.float64)
    return np.moveaxis((codes * scale).reshape(v.shape), -1, axis)


WIDE = False


def mx_kscale(k):
    if not WIDE:
        return np.ones(k)
    levels = np.array([10, -10, 5, -5, 0])
    if k % 512:
        return np.exp2(np.random.permutation(np.resize(levels, k // 32))).repeat(32)
    a = np.empty((k // 512, 16))
    for p in range(k // 512):
        a[p, :8] = np.random.permutation(np.resize(levels, 8))
        for g in range(8):
            far = levels[np.abs(levels - a[p, g]) >= 10]
            a[p, g + 8] = far[np.random.randint(len(far))]
    return np.exp2(a.ravel()).repeat(32)


def f64(x):
    return np.asarray(x).astype(np.float64)


def striped(idx):
    return np.tile(idx.reshape(-1, 16).T, (8, 1)).astype(np.uint16)


def unstriped(offs):
    return offs[:16].T.reshape(-1).astype(np.int64)


E2M1 = np.array([0.0, 0.5, 1.0, 1.5, 2.0, 3.0, 4.0, 6.0, -0.0, -0.5, -1.0, -1.5, -2.0, -3.0, -4.0, -6.0])


def pack_weight(w, fmt):
    k, n = w.shape
    w = f64(np.asarray(w, np.float32).astype(ml_dtypes.bfloat16)).reshape(k // 32, 32, n)
    amax = np.abs(w).max(1)
    if fmt == "e4m3":
        byte = np.frexp(amax)[1] - 1 + 127 - 7
    else:
        mant, ex = np.frexp(amax / 6.0)
        byte = np.where(mant > 0.5, ex, ex - 1) + 127
    byte = np.clip(np.where(amax > 0, byte, 1), 1, 254)
    scaled = (w * np.exp2(127.0 - byte)[:, None, :]).reshape(k, n).astype(np.float32)
    by_word = np.ascontiguousarray(scaled.reshape(k // 512, 128, 4, n).transpose(0, 1, 3, 2))
    if fmt == "e4m3":
        words = by_word.astype(ml_dtypes.float8_e4m3fn).view(np.uint8)
    else:
        c = by_word.astype(ml_dtypes.float4_e2m1fn).view(np.uint8) & 0xF
        words = (c[..., 0::2] | (c[..., 1::2] << 4)).reshape(k // 512, 128, 2 * n)
    return np.ascontiguousarray(words), np.ascontiguousarray(byte.astype(np.uint8).reshape(k // 512, 16, n))


def unpack_weight(words, scales, fmt):
    g, _, n = scales.shape
    words = np.ascontiguousarray(words).reshape(g, 128, n, -1)
    if fmt == "e4m3":
        vals = words.view(ml_dtypes.float8_e4m3fn).astype(np.float64)
    else:
        nib = np.empty((g, 128, n, 4), np.uint8)
        nib[..., 0::2] = words & 0xF
        nib[..., 1::2] = words >> 4
        vals = E2M1[nib]
    vals = vals * np.repeat(np.exp2(scales.astype(np.float64) - 127.0), 8, axis=1)[..., None]
    return vals.transpose(0, 1, 3, 2).reshape(g * 512, n)


def pack_table(v):
    words, scales = pack_weight(v, "e4m3")
    return np.concatenate([words.reshape(words.shape[0], -1), scales.reshape(scales.shape[0], -1)], axis=1)


def unpack_table(tab):
    g, t = tab.shape[0], tab.shape[1] // 528
    return unpack_weight(tab[:, :512 * t].reshape(g, 128, t, 4), tab[:, 512 * t:].reshape(g, 16, t), "e4m3")


K, H, M, T, S = 1536, 512, 1024, 4096, 2048


def setup_inputs():
    n = np.random.standard_normal
    s = mx_kscale(K)[:, None]
    u = mx_kscale(H)[:, None]
    p_w2 = pack_weight(1.4 * n((H, M)) / np.sqrt(H) / u, "e2m1")
    return {
        "tab": pack_table(n((K, T)) * s),
        "w1": (n((K, H)) / np.sqrt(K) / s * u.T).astype(np.float32),
        "w2_words": p_w2[0],
        "w2_scales": p_w2[1],
        "offs": striped(np.random.permutation(T)[:S]),
    }


def reference(tab, w1, w2_words, w2_scales, offs):
    tab_ = unpack_table(tab)[:, unstriped(offs)]
    w1_ = mxq(f64(w1), 0, "e4m3")
    w2_ = unpack_weight(w2_words, w2_scales, "e2m1")
    h_ = mxq(np.maximum(w1_.T @ tab_, 0.0), 0, "e4m3")
    y = h_.T @ w2_
    return y

@@ -1,0 +1,272 @@
+from contextlib import ExitStack
+
+import concourse.mybir as mybir
+
+K, H, M, T, S = 1536, 512, 1024, 4096, 2048
+FLOPS = 2 * S * (K * H + H * M)
+
+F32 = mybir.dt.float32
+BF16 = mybir.dt.bfloat16
+I32 = mybir.dt.int32
+U32 = mybir.dt.uint32
+U16 = mybir.dt.uint16
+U8 = mybir.dt.uint8
+E4M3 = mybir.dt.float8_e4m3fn_x4
+E2M1 = mybir.dt.float4_e2m1fn_x4
+RELU = mybir.ActivationFunctionType.Relu
+
+P = 128
+PASSES = K // 512
+SL = 512
+JT = 128
+
+
+def tile_list_tabmlp_tm_none_kernel(tc, tab, w1, w2_words, w2_scales, offs, out):
+    nc = tc.nc
+    with ExitStack() as ctx:
+        keep = ctx.enter_context(tc.tile_pool(name="keep", bufs=1))
+        ring = ctx.enter_context(tc.tile_pool(name="ring", bufs=4))
+        psum = ctx.enter_context(tc.psum_pool(name="psum", bufs=4))
+
+        lst = keep.tile([P, S // 16], U16, name="lst")
+        nc.sync.dma_start(lst[:], offs)
+
+        table = [keep.tile([P, T], I32, name="table%d" % a, align_bytes=64) for a in range(PASSES)]
+        raw = [keep.tile([P, 4, H], F32, name="raw%d" % a, align_bytes=64) for a in range(PASSES)]
+        planes = keep.tile([P, T], U8, name="planes", align_bytes=64)
+        w2c = keep.tile([P, 2 * M], U8, name="w2c", align_bytes=64)
+        w2s = keep.tile([P, M], U8, name="w2s", align_bytes=64)
+
+        nc.vector.memset(planes[:].bitcast(I32), 0)
+        nc.gpsimd.memset(w2s[:].bitcast(I32), 0)
+
+        def load_table(a):
+            nc.sync.dma_start(table[a][:], tab[a, 0 : 512 * T].rearrange("(p w) -> p w", p=P).bitcast(I32))
+
+        def load_w1(a, c0, c1):
+            nc.sync.dma_start(
+                raw[a][:, :, c0:c1], w1[512 * a : 512 * a + 512, c0:c1].rearrange("(p j) c -> p j c", j=4)
+            )
+
+        def load_scales(queue, q):
+            queue.dma_start(
+                planes[32 * q : 32 * q + 4 * PASSES, :].bitcast(I32),
+                tab[:, 512 * T + 4 * T * q : 512 * T + 4 * T * (q + 1)].rearrange("a (r t) -> a r t", r=4).bitcast(I32),
+            )
+
+        load_scales(nc.scalar, 0)
+        load_scales(nc.scalar, 1)
+        load_table(0)
+        load_scales(nc.sync, 2)
+        load_scales(nc.sync, 3)
+        load_w1(0, 0, H)
+        load_table(1)
+        load_w1(1, 0, H)
+        for q in range(4):
+            nc.sync.dma_start(w2s[32 * q : 32 * q + 4, :].bitcast(I32), w2_scales[0, 4 * q : 4 * q + 4, :].bitcast(I32))
+        load_w1(2, 0, H)
+        load_table(2)
+        nc.sync.dma_start(w2c[:].bitcast(I32), w2_words[0].bitcast(I32))
+
+        gsc = keep.tile([P, S], U8, name="gsc", align_bytes=64)
+        words = {}
+        grouped = [keep.tile([P, 4 * H], BF16, name="grouped%d" % a, align_bytes=64) for a in range(PASSES)]
+        w1c = [keep.tile([P, H], U32, name="w1c%d" % a, align_bytes=64) for a in range(PASSES)]
+        w1s = [keep.tile([P, H], U8, name="w1s%d" % a, align_bytes=64) for a in range(PASSES)]
+        hc = keep.tile([P, S], U32, name="hc", align_bytes=64)
+        hs = keep.tile([P, S], U8, name="hs", align_bytes=64)
+
+        def gather_scales(s):
+            nc.vector.tensor_copy(gsc[:, SL * s : SL * s + SL], planes[:].indirect(lst[:, SL // 16 * s : SL // 16 * (s + 1)]))
+
+        def gather_words(a, s, tag=None):
+            words[a, s] = keep.tile([P, SL], U32, name=tag or "words%d%d" % (a, s), align_bytes=64)
+            nc.vector.tensor_copy(
+                words[a, s][:], table[a][:].bitcast(U32).indirect(lst[:, SL // 16 * s : SL // 16 * (s + 1)])
+            )
+
+        def group_w1(a, m0, m1, copy):
+            copy(
+                out=grouped[a][:].rearrange("p (t m j) -> p m t j", t=4, j=4)[:, m0:m1],
+                in_=raw[a][:].rearrange("p j (m t) -> p m t j", t=4)[:, m0:m1],
+            )
+
+        def quantize_w1(a, c0, c1):
+            nc.vector.quantize_mx(
+                out=w1c[a][:, c0:c1].bitcast(E4M3), scales=w1s[a][:, c0:c1], in_=grouped[a][:, 4 * c0 : 4 * c1]
+            )
+
+        def relu(engine, out, in_):
+            if engine == "S":
+                nc.scalar.activation(out, in_, RELU)
+            else:
+                nc.vector.tensor_scalar_max(out, in_, 0.0)
+
+        def product1(bank, a, t, s, j0, n, first=None, last=None):
+            nc.tensor.matmul_mx(
+                out=bank,
+                lhsT=w1c[a][:, 128 * t : 128 * t + 128].bitcast(E4M3),
+                lhsT_scale=w1s[a][:, 128 * t : 128 * t + 128],
+                rhs=words[a, s][:, j0 : j0 + n].bitcast(E4M3),
+                rhs_scale=gsc[4 * a : P, SL * s + j0 : SL * s + j0 + n],
+                start=(a == 0) if first is None else first,
+                stop=(a == PASSES - 1) if last is None else last,
+            )
+
+        def quantize_h(i):
+            nc.vector.quantize_mx(
+                out=hc[:, JT * i : JT * i + JT].bitcast(E4M3), scales=hs[:, JT * i : JT * i + JT], in_=hgs[i][:]
+            )
+
+        hgs = {}
+
+        def early_h(i):
+            s, c = divmod(i, 4)
+            hg = ring.tile([P, 4 * JT], BF16, name="hg", align_bytes=64, bufs=6)
+            nc.vector.tensor_copy(
+                hg[:].rearrange("p (j t) -> p j t", t=4), hrs[s][:, :, JT * c : JT * c + JT].rearrange("p t j -> p j t")
+            )
+            hgs[i] = hg
+
+        def late_h(i, engine="S"):
+            acc = psum.tile([P, 4, JT], F32, name="late")
+            s, c = divmod(i, 4)
+            for t in range(4):
+                for a in (2, 0, 1):
+                    product1(acc[:, t, :], a, t, s, JT * c, JT, a == 2, a == 1)
+            hg = ring.tile([P, 4 * JT], BF16, name="hg", align_bytes=64, bufs=6)
+            relu(engine, hg[:].rearrange("p (j t) -> p j t", t=4), acc[:].rearrange("p t j -> p j t"))
+            hgs[i] = hg
+
+        def product2(i, engines="SV"):
+            ot = ring.tile([P, M], F32, name="ot", align_bytes=64, bufs=8)
+            for n in range(2):
+                res = psum.tile([P, 512], F32, name="acc")
+                nc.tensor.matmul_mx(
+                    out=res[:],
+                    lhsT=hc[:, JT * i : JT * i + JT].bitcast(E4M3),
+                    lhsT_scale=hs[:, JT * i : JT * i + JT],
+                    rhs=w2c[:, 1024 * n : 1024 * n + 1024].bitcast(E2M1),
+                    rhs_scale=w2s[:, 512 * n : 512 * n + 512],
+                    start=True,
+                    stop=True,
+                )
+                if engines[n] == "S":
+                    nc.scalar.copy(out=ot[:, 512 * n : 512 * n + 512], in_=res[:])
+                else:
+                    nc.vector.tensor_copy(ot[:, 512 * n : 512 * n + 512], res[:])
+            nc.sync.dma_start(out[JT * i : JT * i + JT, :], ot[:])
+
+        banks = []
+        for s in range(2):
+            for t in range(4):
+                b = psum.tile([P, SL], F32, name="acc" if s == 0 else "late")
+                banks.append(b)
+        gather_scales(0)
+        gather_scales(1)
+        gather_scales(2)
+        gather_scales(3)
+        group_w1(0, 0, 128, nc.scalar.copy)
+        quantize_w1(0, 0, H)
+        gather_words(0, 0)
+        gather_words(0, 1)
+        gather_words(0, 2)
+        gather_words(0, 3)
+        product1(banks[0][:], 0, 0, 0, 0, SL)
+        product1(banks[1][:], 0, 1, 0, 0, SL)
+        product1(banks[2][:], 0, 2, 0, 0, SL)
+        product1(banks[3][:], 0, 3, 0, 0, SL)
+        product1(banks[4][:], 0, 0, 1, 0, SL)
+        product1(banks[5][:], 0, 1, 1, 0, SL)
+        product1(banks[6][:], 0, 2, 1, 0, SL)
+        product1(banks[7][:], 0, 3, 1, 0, SL)
+        gather_words(1, 0)
+        gather_words(1, 1)
+        gather_words(1, 2)
+        gather_words(1, 3)
+        group_w1(1, 0, 128, nc.scalar.copy)
+        quantize_w1(1, 0, H)
+        product1(banks[0][:], 1, 0, 0, 0, SL)
+        product1(banks[1][:], 1, 1, 0, 0, SL)
+        product1(banks[2][:], 1, 2, 0, 0, SL)
+        product1(banks[3][:], 1, 3, 0, 0, SL)
+        product1(banks[4][:], 1, 0, 1, 0, SL)
+        product1(banks[5][:], 1, 1, 1, 0, SL)
+        product1(banks[6][:], 1, 2, 1, 0, SL)
+        product1(banks[7][:], 1, 3, 1, 0, SL)
+        group_w1(2, 0, 64, nc.scalar.copy)
+        group_w1(2, 64, 128, nc.scalar.copy)
+        quantize_w1(2, 0, H)
+        hrs = [ring.tile([P, 4, SL], BF16, name="hr", align_bytes=64) for s in range(2)]
+        gather_words(2, 0)
+        product1(banks[0][:], 2, 0, 0, 0, SL)
+        product1(banks[1][:], 2, 1, 0, 0, SL)
+        product1(banks[2][:], 2, 2, 0, 0, SL)
+        product1(banks[3][:], 2, 3, 0, 0, SL)
+        relu("S", hrs[0][:, 0, 0:128], banks[0][:, 0:128])
+        relu("S", hrs[0][:, 1, 0:128], banks[1][:, 0:128])
+        relu("S", hrs[0][:, 2, 0:128], banks[2][:, 0:128])
+        relu("S", hrs[0][:, 3, 0:128], banks[3][:, 0:128])
+        early_h(0)
+        quantize_h(0)
+        product2(0)
+        gather_words(2, 1)
+        product1(banks[4][:], 2, 0, 1, 0, SL)
+        product1(banks[5][:], 2, 1, 1, 0, SL)
+        product1(banks[6][:], 2, 2, 1, 0, SL)
+        product1(banks[7][:], 2, 3, 1, 0, SL)
+        relu("S", hrs[0][:, 0, 128:512], banks[0][:, 128:512])
+        relu("V", hrs[0][:, 1, 128:512], banks[1][:, 128:512])
+        relu("S", hrs[0][:, 2, 128:512], banks[2][:, 128:512])
+        relu("V", hrs[0][:, 3, 128:512], banks[3][:, 128:512])
+        early_h(1)
+        early_h(2)
+        quantize_h(1)
+        product2(1)
+        early_h(3)
+        quantize_h(2)
+        product2(2)
+        quantize_h(3)
+        relu("S", hrs[1][:, 0, 0:SL], banks[4][:, 0:SL])
+        relu("S", hrs[1][:, 1, 0:SL], banks[5][:, 0:SL])
+        product2(3)
+        gather_words(2, 2, tag="words20")
+        relu("S", hrs[1][:, 2, 0:SL], banks[6][:, 0:SL])
+        relu("S", hrs[1][:, 3, 0:SL], banks[7][:, 0:SL])
+        early_h(4)
+        early_h(5)
+        quantize_h(4)
+        late_h(8)
+        product2(4)
+        early_h(6)
+        quantize_h(5)
+        product2(5)
+        early_h(7)
+        quantize_h(6)
+        gather_words(2, 3, tag="words21")
+        quantize_h(8)
+        quantize_h(7)
+        late_h(9)
+        product2(6)
+        late_h(10)
+        product2(7)
+        quantize_h(9)
+        product2(8)
+        late_h(11)
+        quantize_h(10)
+        product2(9)
+        late_h(12)
+        quantize_h(11)
+        product2(10)
+        late_h(13)
+        quantize_h(12)
+        product2(11)
+        late_h(14)
+        quantize_h(13)
+        product2(12)
+        late_h(15)
+        quantize_h(14)
+        product2(13)
+        quantize_h(15)
+        product2(14)
+        product2(15)

@@ -14,19 +14,24 @@ U8 = mybir.dt.uint8
 E4M3 = mybir.dt.float8_e4m3fn_x4
 E2M1 = mybir.dt.float4_e2m1fn_x4
 RELU = mybir.ActivationFunctionType.Relu
+COPY = mybir.ActivationFunctionType.Copy
 
 P = 128
 PASSES = K // 512
+LAST = PASSES - 1
 SL = 512
 JT = 128
+TILES = S // JT
+BANKS = 8
+RING = 4
 
 
 def tile_list_tabmlp_tm_none_kernel(tc, tab, w1, w2_words, w2_scales, offs, out):
     nc = tc.nc
     with ExitStack() as ctx:
         keep = ctx.enter_context(tc.tile_pool(name="keep", bufs=1))
-        ring = ctx.enter_context(tc.tile_pool(name="ring", bufs=4))
-        psum = ctx.enter_context(tc.psum_pool(name="psum", bufs=4))
+        ring = ctx.enter_context(tc.tile_pool(name="ring", bufs=10))
+        psum = ctx.enter_context(tc.psum_pool(name="psum", bufs=1))
 
         lst = keep.tile([P, S // 16], U16, name="lst")
         nc.sync.dma_start(lst[:], offs)
@@ -38,235 +43,157 @@ def tile_list_tabmlp_tm_none_kernel(tc, tab, w1, w2_words, w2_scales, offs, out)
         w2s = keep.tile([P, M], U8, name="w2s", align_bytes=64)
 
         nc.vector.memset(planes[:].bitcast(I32), 0)
-        nc.gpsimd.memset(w2s[:].bitcast(I32), 0)
 
         def load_table(a):
             nc.sync.dma_start(table[a][:], tab[a, 0 : 512 * T].rearrange("(p w) -> p w", p=P).bitcast(I32))
 
-        def load_w1(a, c0, c1):
-            nc.sync.dma_start(
-                raw[a][:, :, c0:c1], w1[512 * a : 512 * a + 512, c0:c1].rearrange("(p j) c -> p j c", j=4)
-            )
+        def load_w1(a):
+            nc.sync.dma_start(raw[a][:], w1[512 * a : 512 * a + 512, :].rearrange("(p j) c -> p j c", j=4))
 
-        def load_scales(queue, q):
-            queue.dma_start(
-                planes[32 * q : 32 * q + 4 * PASSES, :].bitcast(I32),
-                tab[:, 512 * T + 4 * T * q : 512 * T + 4 * T * (q + 1)].rearrange("a (r t) -> a r t", r=4).bitcast(I32),
-            )
+        def load_scales():
+            for q in range(4):
+                nc.sync.dma_start(
+                    planes[32 * q : 32 * q + 4 * PASSES, :].bitcast(I32),
+                    tab[:, 512 * T + 4 * T * q : 512 * T + 4 * T * (q + 1)].rearrange("a (r t) -> a r t", r=4).bitcast(I32),
+                )
 
-        load_scales(nc.scalar, 0)
-        load_scales(nc.scalar, 1)
+        nc.gpsimd.memset(w2s[:].bitcast(I32), 0)
         load_table(0)
-        load_scales(nc.sync, 2)
-        load_scales(nc.sync, 3)
-        load_w1(0, 0, H)
+        load_scales()
+        load_w1(0)
         load_table(1)
-        load_w1(1, 0, H)
-        for q in range(4):
-            nc.sync.dma_start(w2s[32 * q : 32 * q + 4, :].bitcast(I32), w2_scales[0, 4 * q : 4 * q + 4, :].bitcast(I32))
-        load_w1(2, 0, H)
+        load_w1(1)
+        load_w1(2)
         load_table(2)
         nc.sync.dma_start(w2c[:].bitcast(I32), w2_words[0].bitcast(I32))
+        for q in range(4):
+            nc.sync.dma_start(w2s[32 * q : 32 * q + 4, :].bitcast(I32), w2_scales[0, 4 * q : 4 * q + 4, :].bitcast(I32))
 
         gsc = keep.tile([P, S], U8, name="gsc", align_bytes=64)
-        words = {}
-        grouped = [keep.tile([P, 4 * H], BF16, name="grouped%d" % a, align_bytes=64) for a in range(PASSES)]
         w1c = [keep.tile([P, H], U32, name="w1c%d" % a, align_bytes=64) for a in range(PASSES)]
         w1s = [keep.tile([P, H], U8, name="w1s%d" % a, align_bytes=64) for a in range(PASSES)]
-        hc = keep.tile([P, S], U32, name="hc", align_bytes=64)
+        hc = {}
         hs = keep.tile([P, S], U8, name="hs", align_bytes=64)
+        words = {}
+        acc = {}
+        hidden = {}
+
+        def slice_of_list(s):
+            return lst[:, SL // 16 * s : SL // 16 * (s + 1)]
 
         def gather_scales(s):
-            nc.vector.tensor_copy(gsc[:, SL * s : SL * s + SL], planes[:].indirect(lst[:, SL // 16 * s : SL // 16 * (s + 1)]))
+            nc.vector.tensor_copy(gsc[:, SL * s : SL * s + SL], planes[:].indirect(slice_of_list(s)))
 
-        def gather_words(a, s, tag=None):
-            words[a, s] = keep.tile([P, SL], U32, name=tag or "words%d%d" % (a, s), align_bytes=64)
-            nc.vector.tensor_copy(
-                words[a, s][:], table[a][:].bitcast(U32).indirect(lst[:, SL // 16 * s : SL // 16 * (s + 1)])
+        def gather_words(a, s, slot=None, into=None):
+            if into is None:
+                into = keep.tile([P, SL], U32, name=slot or "words%d%d" % (a, s), align_bytes=64)[:]
+            words[a, s] = into
+            nc.vector.tensor_copy(into, table[a][:].bitcast(U32).indirect(slice_of_list(s)))
+
+        def quantize_w1(a):
+            grouped = keep.tile([P, 4 * H], BF16, name="grouped%d" % a, align_bytes=64)
+            nc.scalar.activation(
+                grouped[:].rearrange("p (t m j) -> p m t j", t=4, j=4),
+                raw[a][:].rearrange("p j (m t) -> p m t j", t=4),
+                COPY,
             )
+            nc.vector.quantize_mx(out=w1c[a][:].bitcast(E4M3), scales=w1s[a][:], in_=grouped[:])
 
-        def group_w1(a, m0, m1, copy):
-            copy(
-                out=grouped[a][:].rearrange("p (t m j) -> p m t j", t=4, j=4)[:, m0:m1],
-                in_=raw[a][:].rearrange("p j (m t) -> p m t j", t=4)[:, m0:m1],
-            )
+        def product1(i, a):
+            if a == 0:
+                bank = i if i < BANKS else RING + i % (BANKS - RING)
+                acc[i] = psum.tile([P, 4, JT], F32, name="bank%d" % bank)
+            s, c = divmod(i, SL // JT)
+            for t in range(4):
+                nc.tensor.matmul_mx(
+                    out=acc[i][:, t, :],
+                    lhsT=w1c[a][:, 128 * t : 128 * t + 128].bitcast(E4M3),
+                    lhsT_scale=w1s[a][:, 128 * t : 128 * t + 128],
+                    rhs=words[a, s][:, JT * c : JT * c + JT].bitcast(E4M3),
+                    rhs_scale=gsc[4 * a : P, JT * i : JT * i + JT],
+                    start=(a == 0 and t == 0),
+                    stop=(a == LAST and t == 3),
+                )
 
-        def quantize_w1(a, c0, c1):
-            nc.vector.quantize_mx(
-                out=w1c[a][:, c0:c1].bitcast(E4M3), scales=w1s[a][:, c0:c1], in_=grouped[a][:, 4 * c0 : 4 * c1]
-            )
-
-        def relu(engine, out, in_):
-            if engine == "S":
-                nc.scalar.activation(out, in_, RELU)
+        def relu(i):
+            if i in hidden or i >= TILES:
+                return
+            hidden[i] = keep.tile([P, 4 * JT], BF16, name="hidden%d" % i, align_bytes=64)
+            dst = hidden[i][:].rearrange("p (j t) -> p j t", t=4)
+            src = acc[i][:].rearrange("p t j -> p j t")
+            if i in (3, 6, 9, 12):
+                nc.vector.tensor_scalar_max(dst, src, 0.0)
             else:
-                nc.vector.tensor_scalar_max(out, in_, 0.0)
-
-        def product1(bank, a, t, s, j0, n, first=None, last=None):
-            nc.tensor.matmul_mx(
-                out=bank,
-                lhsT=w1c[a][:, 128 * t : 128 * t + 128].bitcast(E4M3),
-                lhsT_scale=w1s[a][:, 128 * t : 128 * t + 128],
-                rhs=words[a, s][:, j0 : j0 + n].bitcast(E4M3),
-                rhs_scale=gsc[4 * a : P, SL * s + j0 : SL * s + j0 + n],
-                start=(a == 0) if first is None else first,
-                stop=(a == PASSES - 1) if last is None else last,
-            )
+                nc.scalar.activation(dst, src, RELU)
 
         def quantize_h(i):
+            hc[i] = keep.tile([P, JT], U32, name="hc%d" % i, align_bytes=64)
             nc.vector.quantize_mx(
-                out=hc[:, JT * i : JT * i + JT].bitcast(E4M3), scales=hs[:, JT * i : JT * i + JT], in_=hgs[i][:]
+                out=hc[i][:].bitcast(E4M3), scales=hs[:, JT * i : JT * i + JT], in_=hidden[i][:]
             )
 
-        hgs = {}
-
-        def early_h(i):
-            s, c = divmod(i, 4)
-            hg = ring.tile([P, 4 * JT], BF16, name="hg", align_bytes=64, bufs=6)
-            nc.vector.tensor_copy(
-                hg[:].rearrange("p (j t) -> p j t", t=4), hrs[s][:, :, JT * c : JT * c + JT].rearrange("p t j -> p j t")
-            )
-            hgs[i] = hg
-
-        def late_h(i, engine="S"):
-            acc = psum.tile([P, 4, JT], F32, name="late")
-            s, c = divmod(i, 4)
-            for t in range(4):
-                for a in (2, 0, 1):
-                    product1(acc[:, t, :], a, t, s, JT * c, JT, a == 2, a == 1)
-            hg = ring.tile([P, 4 * JT], BF16, name="hg", align_bytes=64, bufs=6)
-            relu(engine, hg[:].rearrange("p (j t) -> p j t", t=4), acc[:].rearrange("p t j -> p j t"))
-            hgs[i] = hg
-
-        def product2(i, engines="SV"):
-            ot = ring.tile([P, M], F32, name="ot", align_bytes=64, bufs=8)
+        def product2(i):
+            ot = ring.tile([P, M], F32, name="ot", align_bytes=64)
             for n in range(2):
-                res = psum.tile([P, 512], F32, name="acc")
+                res = psum.tile([P, 512], F32, name="bank%d" % ((2 * i + n) % RING))
                 nc.tensor.matmul_mx(
                     out=res[:],
-                    lhsT=hc[:, JT * i : JT * i + JT].bitcast(E4M3),
+                    lhsT=hc[i][:].bitcast(E4M3),
                     lhsT_scale=hs[:, JT * i : JT * i + JT],
                     rhs=w2c[:, 1024 * n : 1024 * n + 1024].bitcast(E2M1),
                     rhs_scale=w2s[:, 512 * n : 512 * n + 512],
                     start=True,
                     stop=True,
                 )
-                if engines[n] == "S":
+                if (n == 0 and i not in ()) or i in (1, 5):
                     nc.scalar.copy(out=ot[:, 512 * n : 512 * n + 512], in_=res[:])
                 else:
                     nc.vector.tensor_copy(ot[:, 512 * n : 512 * n + 512], res[:])
-            nc.sync.dma_start(out[JT * i : JT * i + JT, :], ot[:])
+                if i < 0:
+                    nc.sync.dma_start(out[JT * i : JT * i + JT, 512 * n : 512 * n + 512], ot[:, 512 * n : 512 * n + 512])
+            if i >= 0:
+                nc.sync.dma_start(out[JT * i : JT * i + JT, :], ot[:])
 
-        banks = []
-        for s in range(2):
-            for t in range(4):
-                b = psum.tile([P, SL], F32, name="acc" if s == 0 else "late")
-                banks.append(b)
-        gather_scales(0)
-        gather_scales(1)
-        gather_scales(2)
-        gather_scales(3)
-        group_w1(0, 0, 128, nc.scalar.copy)
-        quantize_w1(0, 0, H)
-        gather_words(0, 0)
-        gather_words(0, 1)
-        gather_words(0, 2)
-        gather_words(0, 3)
-        product1(banks[0][:], 0, 0, 0, 0, SL)
-        product1(banks[1][:], 0, 1, 0, 0, SL)
-        product1(banks[2][:], 0, 2, 0, 0, SL)
-        product1(banks[3][:], 0, 3, 0, 0, SL)
-        product1(banks[4][:], 0, 0, 1, 0, SL)
-        product1(banks[5][:], 0, 1, 1, 0, SL)
-        product1(banks[6][:], 0, 2, 1, 0, SL)
-        product1(banks[7][:], 0, 3, 1, 0, SL)
-        gather_words(1, 0)
-        gather_words(1, 1)
-        gather_words(1, 2)
-        gather_words(1, 3)
-        group_w1(1, 0, 128, nc.scalar.copy)
-        quantize_w1(1, 0, H)
-        product1(banks[0][:], 1, 0, 0, 0, SL)
-        product1(banks[1][:], 1, 1, 0, 0, SL)
-        product1(banks[2][:], 1, 2, 0, 0, SL)
-        product1(banks[3][:], 1, 3, 0, 0, SL)
-        product1(banks[4][:], 1, 0, 1, 0, SL)
-        product1(banks[5][:], 1, 1, 1, 0, SL)
-        product1(banks[6][:], 1, 2, 1, 0, SL)
-        product1(banks[7][:], 1, 3, 1, 0, SL)
-        group_w1(2, 0, 64, nc.scalar.copy)
-        group_w1(2, 64, 128, nc.scalar.copy)
-        quantize_w1(2, 0, H)
-        hrs = [ring.tile([P, 4, SL], BF16, name="hr", align_bytes=64) for s in range(2)]
-        gather_words(2, 0)
-        product1(banks[0][:], 2, 0, 0, 0, SL)
-        product1(banks[1][:], 2, 1, 0, 0, SL)
-        product1(banks[2][:], 2, 2, 0, 0, SL)
-        product1(banks[3][:], 2, 3, 0, 0, SL)
-        relu("S", hrs[0][:, 0, 0:128], banks[0][:, 0:128])
-        relu("S", hrs[0][:, 1, 0:128], banks[1][:, 0:128])
-        relu("S", hrs[0][:, 2, 0:128], banks[2][:, 0:128])
-        relu("S", hrs[0][:, 3, 0:128], banks[3][:, 0:128])
-        early_h(0)
+        for s in range(4):
+            gather_scales(s)
+        for s in range(4):
+            gather_words(0, s)
+        quantize_w1(0)
+        for i in range(BANKS):
+            product1(i, 0)
+        middle = keep.tile([P, 3 * SL], U32, name="planes", align_bytes=64)
+        for s in range(3):
+            gather_words(1, s, into=middle[:, SL * s : SL * s + SL])
+        quantize_w1(1)
+        gather_words(1, 3, "grouped1")
+        for i in range(BANKS):
+            product1(i, 1)
+        quantize_w1(LAST)
+
+        front = keep.tile([P, 2 * SL], U32, name="grouped%d" % LAST, align_bytes=64)
+        gather_words(LAST, 0, into=front[:, 0:SL])
+        for i in range(4):
+            product1(i, LAST)
+        gather_words(LAST, 1, into=front[:, SL : 2 * SL])
+        relu(0)
         quantize_h(0)
-        product2(0)
-        gather_words(2, 1)
-        product1(banks[4][:], 2, 0, 1, 0, SL)
-        product1(banks[5][:], 2, 1, 1, 0, SL)
-        product1(banks[6][:], 2, 2, 1, 0, SL)
-        product1(banks[7][:], 2, 3, 1, 0, SL)
-        relu("S", hrs[0][:, 0, 128:512], banks[0][:, 128:512])
-        relu("V", hrs[0][:, 1, 128:512], banks[1][:, 128:512])
-        relu("S", hrs[0][:, 2, 128:512], banks[2][:, 128:512])
-        relu("V", hrs[0][:, 3, 128:512], banks[3][:, 128:512])
-        early_h(1)
-        early_h(2)
-        quantize_h(1)
-        product2(1)
-        early_h(3)
-        quantize_h(2)
-        product2(2)
-        quantize_h(3)
-        relu("S", hrs[1][:, 0, 0:SL], banks[4][:, 0:SL])
-        relu("S", hrs[1][:, 1, 0:SL], banks[5][:, 0:SL])
-        product2(3)
-        gather_words(2, 2, tag="words20")
-        relu("S", hrs[1][:, 2, 0:SL], banks[6][:, 0:SL])
-        relu("S", hrs[1][:, 3, 0:SL], banks[7][:, 0:SL])
-        early_h(4)
-        early_h(5)
-        quantize_h(4)
-        late_h(8)
-        product2(4)
-        early_h(6)
-        quantize_h(5)
-        product2(5)
-        early_h(7)
-        quantize_h(6)
-        gather_words(2, 3, tag="words21")
-        quantize_h(8)
-        quantize_h(7)
-        late_h(9)
-        product2(6)
-        late_h(10)
-        product2(7)
-        quantize_h(9)
-        product2(8)
-        late_h(11)
-        quantize_h(10)
-        product2(9)
-        late_h(12)
-        quantize_h(11)
-        product2(10)
-        late_h(13)
-        quantize_h(12)
-        product2(11)
-        late_h(14)
-        quantize_h(13)
-        product2(12)
-        late_h(15)
-        quantize_h(14)
-        product2(13)
-        quantize_h(15)
-        product2(14)
-        product2(15)
+        relu(1)
+        late_at = {2 + (3 * n) // 2: BANKS + n for n in range(TILES - BANKS)}
+        for i in range(TILES):
+            product2(i)
+            if i == 0:
+                gather_words(LAST, 2, "hc%d" % i)
+            if i == 4:
+                gather_words(LAST, 3, "hc%d" % i)
+            if i < 2:
+                relu(2 * i + 2)
+                product1(2 * i + 4, LAST)
+                product1(2 * i + 5, LAST)
+                relu(3)
+            relu(i + 1)
+            if i + 1 < TILES:
+                quantize_h(i + 1)
+            if i in late_at:
+                relu(late_at[i] - (BANKS - RING))
+                for a in range(PASSES):
+                    product1(late_at[i], a)

@@ -38,11 +38,16 @@ def tile_list_tabmlp_tm_none_kernel(tc, tab, w1, w2_words, w2_scales, offs, out)
 
         table = [keep.tile([P, T], I32, name="table%d" % a, align_bytes=64) for a in range(PASSES)]
         raw = [keep.tile([P, 4, H], F32, name="raw%d" % a, align_bytes=64) for a in range(PASSES)]
-        planes = keep.tile([P, T], U8, name="planes", align_bytes=64)
         w2c = keep.tile([P, 2 * M], U8, name="w2c", align_bytes=64)
         w2s = keep.tile([P, M], U8, name="w2s", align_bytes=64)
-
-        nc.vector.memset(planes[:].bitcast(I32), 0)
+        gsc = keep.tile([P, S], U8, name="gsc", align_bytes=64)
+        w1c = [keep.tile([P, H], U32, name="w1c%d" % a, align_bytes=64) for a in range(PASSES)]
+        hs = keep.tile([P, S], U8, name="hs", align_bytes=64)
+        first = keep.tile([P, S], U32, name="first", align_bytes=64)
+        hc = {}
+        words = {}
+        acc = {}
+        hidden = {}
 
         def load_table(a):
             nc.sync.dma_start(table[a][:], tab[a, 0 : 512 * T].rearrange("(p w) -> p w", p=P).bitcast(I32))
@@ -50,45 +55,39 @@ def tile_list_tabmlp_tm_none_kernel(tc, tab, w1, w2_words, w2_scales, offs, out)
         def load_w1(a):
             nc.sync.dma_start(raw[a][:], w1[512 * a : 512 * a + 512, :].rearrange("(p j) c -> p j c", j=4))
 
-        def load_scales():
+        def entries(s0, s1):
+            return lst[:, SL // 16 * s0 : SL // 16 * s1]
+
+        def gather_words(a, s0, s1, into):
+            for s in range(s0, s1):
+                words[a, s] = into[:, SL * (s - s0) : SL * (s - s0 + 1)]
+            nc.vector.tensor_copy(into, table[a][:].bitcast(U32).indirect(entries(s0, s1)))
+
+        with tc.tile_pool(name="rows", bufs=1) as rows:
+            planes = rows.tile([P, T], U8, name="planes", align_bytes=64)
+            nc.vector.memset(planes[:].bitcast(I32), 0)
+            nc.gpsimd.memset(w2s[:].bitcast(I32), 0)
+            load_table(0)
             for q in range(4):
                 nc.sync.dma_start(
                     planes[32 * q : 32 * q + 4 * PASSES, :].bitcast(I32),
                     tab[:, 512 * T + 4 * T * q : 512 * T + 4 * T * (q + 1)].rearrange("a (r t) -> a r t", r=4).bitcast(I32),
                 )
+            load_w1(0)
+            load_table(1)
+            load_w1(1)
+            load_w1(2)
+            load_table(2)
+            nc.sync.dma_start(w2c[:].bitcast(I32), w2_words[0].bitcast(I32))
+            for q in range(4):
+                nc.sync.dma_start(w2s[32 * q : 32 * q + 4, :].bitcast(I32), w2_scales[0, 4 * q : 4 * q + 4, :].bitcast(I32))
+            gather_words(0, 0, 2, first[:, 0 : 2 * SL])
+            nc.vector.tensor_copy(gsc[:], planes[:].indirect(lst[:]))
 
-        nc.gpsimd.memset(w2s[:].bitcast(I32), 0)
-        load_table(0)
-        load_scales()
-        load_w1(0)
-        load_table(1)
-        load_w1(1)
-        load_w1(2)
-        load_table(2)
-        nc.sync.dma_start(w2c[:].bitcast(I32), w2_words[0].bitcast(I32))
-        for q in range(4):
-            nc.sync.dma_start(w2s[32 * q : 32 * q + 4, :].bitcast(I32), w2_scales[0, 4 * q : 4 * q + 4, :].bitcast(I32))
-
-        gsc = keep.tile([P, S], U8, name="gsc", align_bytes=64)
-        w1c = [keep.tile([P, H], U32, name="w1c%d" % a, align_bytes=64) for a in range(PASSES)]
-        w1s = [keep.tile([P, H], U8, name="w1s%d" % a, align_bytes=64) for a in range(PASSES)]
-        hc = {}
-        hs = keep.tile([P, S], U8, name="hs", align_bytes=64)
-        words = {}
-        acc = {}
-        hidden = {}
-
-        def slice_of_list(s):
-            return lst[:, SL // 16 * s : SL // 16 * (s + 1)]
-
-        def gather_scales(s):
-            nc.vector.tensor_copy(gsc[:, SL * s : SL * s + SL], planes[:].indirect(slice_of_list(s)))
-
-        def gather_words(a, s, slot=None, into=None):
-            if into is None:
-                into = keep.tile([P, SL], U32, name=slot or "words%d%d" % (a, s), align_bytes=64)[:]
-            words[a, s] = into
-            nc.vector.tensor_copy(into, table[a][:].bitcast(U32).indirect(slice_of_list(s)))
+        later = ctx.enter_context(tc.tile_pool(name="later", bufs=1))
+        w1s = later.tile([P, PASSES * H], U8, name="w1s", align_bytes=64)
+        second = later.tile([P, 3 * SL], U32, name="second", align_bytes=64)
+        front = later.tile([P, 2 * SL], U32, name="front", align_bytes=64)
 
         def quantize_w1(a):
             grouped = keep.tile([P, 4 * H], BF16, name="grouped%d" % a, align_bytes=64)
@@ -97,7 +96,7 @@ def tile_list_tabmlp_tm_none_kernel(tc, tab, w1, w2_words, w2_scales, offs, out)
                 raw[a][:].rearrange("p j (m t) -> p m t j", t=4),
                 COPY,
             )
-            nc.vector.quantize_mx(out=w1c[a][:].bitcast(E4M3), scales=w1s[a][:], in_=grouped[:])
+            nc.vector.quantize_mx(out=w1c[a][:].bitcast(E4M3), scales=w1s[:, H * a : H * a + H], in_=grouped[:])
 
         def product1(i, a):
             if a == 0:
@@ -108,7 +107,7 @@ def tile_list_tabmlp_tm_none_kernel(tc, tab, w1, w2_words, w2_scales, offs, out)
                 nc.tensor.matmul_mx(
                     out=acc[i][:, t, :],
                     lhsT=w1c[a][:, 128 * t : 128 * t + 128].bitcast(E4M3),
-                    lhsT_scale=w1s[a][:, 128 * t : 128 * t + 128],
+                    lhsT_scale=w1s[:, H * a + 128 * t : H * a + 128 * t + 128],
                     rhs=words[a, s][:, JT * c : JT * c + JT].bitcast(E4M3),
                     rhs_scale=gsc[4 * a : P, JT * i : JT * i + JT],
                     start=(a == 0 and t == 0),
@@ -127,6 +126,8 @@ def tile_list_tabmlp_tm_none_kernel(tc, tab, w1, w2_words, w2_scales, offs, out)
                 nc.scalar.activation(dst, src, RELU)
 
         def quantize_h(i):
+            if i in hc or i >= TILES:
+                return
             hc[i] = keep.tile([P, JT], U32, name="hc%d" % i, align_bytes=64)
             nc.vector.quantize_mx(
                 out=hc[i][:].bitcast(E4M3), scales=hs[:, JT * i : JT * i + JT], in_=hidden[i][:]
@@ -149,51 +150,49 @@ def tile_list_tabmlp_tm_none_kernel(tc, tab, w1, w2_words, w2_scales, offs, out)
                     nc.scalar.copy(out=ot[:, 512 * n : 512 * n + 512], in_=res[:])
                 else:
                     nc.vector.tensor_copy(ot[:, 512 * n : 512 * n + 512], res[:])
-                if i < 0:
+                if i in (0, 15):
                     nc.sync.dma_start(out[JT * i : JT * i + JT, 512 * n : 512 * n + 512], ot[:, 512 * n : 512 * n + 512])
-            if i >= 0:
+            if i not in (0, 15):
                 nc.sync.dma_start(out[JT * i : JT * i + JT, :], ot[:])
 
-        for s in range(4):
-            gather_scales(s)
-        for s in range(4):
-            gather_words(0, s)
+        def gather_late(s, slot):
+            gather_words(LAST, s, s + 1, keep.tile([P, SL], U32, name=slot, align_bytes=64)[:])
+
+        gather_words(0, 2, 4, first[:, 2 * SL : 4 * SL])
         quantize_w1(0)
         for i in range(BANKS):
             product1(i, 0)
-        middle = keep.tile([P, 3 * SL], U32, name="planes", align_bytes=64)
-        for s in range(3):
-            gather_words(1, s, into=middle[:, SL * s : SL * s + SL])
+        gather_words(1, 0, 3, second[:])
         quantize_w1(1)
-        gather_words(1, 3, "grouped1")
+        gather_words(1, 3, 4, keep.tile([P, SL], U32, name="raw1", align_bytes=64)[:])
         for i in range(BANKS):
             product1(i, 1)
         quantize_w1(LAST)
 
-        front = keep.tile([P, 2 * SL], U32, name="grouped%d" % LAST, align_bytes=64)
-        gather_words(LAST, 0, into=front[:, 0:SL])
+        gather_words(LAST, 0, 1, front[:, 0:SL])
         for i in range(4):
             product1(i, LAST)
-        gather_words(LAST, 1, into=front[:, SL : 2 * SL])
+        gather_words(LAST, 1, 2, front[:, SL : 2 * SL])
         relu(0)
         quantize_h(0)
         relu(1)
-        late_at = {2 + (3 * n) // 2: BANKS + n for n in range(TILES - BANKS)}
+        units = [(i, a) for i in range(BANKS, TILES) for a in range(PASSES)]
         for i in range(TILES):
             product2(i)
             if i == 0:
-                gather_words(LAST, 2, "hc%d" % i)
+                gather_late(2, "hc%d" % i)
             if i == 4:
-                gather_words(LAST, 3, "hc%d" % i)
+                gather_late(3, "hc%d" % i)
             if i < 2:
                 relu(2 * i + 2)
                 product1(2 * i + 4, LAST)
                 product1(2 * i + 5, LAST)
                 relu(3)
             relu(i + 1)
-            if i + 1 < TILES:
-                quantize_h(i + 1)
-            if i in late_at:
-                relu(late_at[i] - (BANKS - RING))
-                for a in range(PASSES):
-                    product1(late_at[i], a)
+            quantize_h(i + 1)
+            for u, a in units[max(0, 9 * (i - 2) // 4) : max(0, 9 * (i - 1) // 4)]:
+                if a == 0:
+                    relu(u - (BANKS - RING))
+                product1(u, a)
+                if a == LAST and u >= 12:
+                    relu(u)

@@ -24,6 +24,8 @@ JT = 128
 TILES = S // JT
 BANKS = 8
 RING = 4
+EARLY = (0, 1, 2, 3, 4, 5, 8, 9)
+LATE = (6, 7, 10, 11, 12, 13, 14, 15)
 
 
 def tile_list_tabmlp_tm_none_kernel(tc, tab, w1, w2_words, w2_scales, offs, out):
@@ -48,6 +50,7 @@ def tile_list_tabmlp_tm_none_kernel(tc, tab, w1, w2_words, w2_scales, offs, out)
         words = {}
         acc = {}
         hidden = {}
+        pending = {}
 
         def load_table(a):
             nc.sync.dma_start(table[a][:], tab[a, 0 : 512 * T].rearrange("(p w) -> p w", p=P).bitcast(I32))
@@ -66,16 +69,16 @@ def tile_list_tabmlp_tm_none_kernel(tc, tab, w1, w2_words, w2_scales, offs, out)
         with tc.tile_pool(name="rows", bufs=1) as rows:
             planes = rows.tile([P, T], U8, name="planes", align_bytes=64)
             nc.vector.memset(planes[:].bitcast(I32), 0)
-            nc.gpsimd.memset(w2s[:].bitcast(I32), 0)
+            nc.vector.memset(w2s[:].bitcast(I32), 0)
             load_table(0)
+            load_w1(0)
             for q in range(4):
                 nc.sync.dma_start(
                     planes[32 * q : 32 * q + 4 * PASSES, :].bitcast(I32),
                     tab[:, 512 * T + 4 * T * q : 512 * T + 4 * T * (q + 1)].rearrange("a (r t) -> a r t", r=4).bitcast(I32),
                 )
-            load_w1(0)
-            load_table(1)
             load_w1(1)
+            load_table(1)
             load_w1(2)
             load_table(2)
             nc.sync.dma_start(w2c[:].bitcast(I32), w2_words[0].bitcast(I32))
@@ -89,24 +92,35 @@ def tile_list_tabmlp_tm_none_kernel(tc, tab, w1, w2_words, w2_scales, offs, out)
         second = later.tile([P, 3 * SL], U32, name="second", align_bytes=64)
         front = later.tile([P, 2 * SL], U32, name="front", align_bytes=64)
 
-        def quantize_w1(a):
-            grouped = keep.tile([P, 4 * H], BF16, name="grouped%d" % a, align_bytes=64)
+        grouped = {}
+        codes = {}
+
+        def round_w1(a):
+            grouped[a] = keep.tile([P, 4 * H], BF16, name="grouped%d" % a, align_bytes=64)
             nc.scalar.activation(
-                grouped[:].rearrange("p (t m j) -> p m t j", t=4, j=4),
+                grouped[a][:].rearrange("p (t m j) -> p m t j", t=4, j=4),
                 raw[a][:].rearrange("p j (m t) -> p m t j", t=4),
                 COPY,
             )
-            nc.vector.quantize_mx(out=w1c[a][:].bitcast(E4M3), scales=w1s[:, H * a : H * a + H], in_=grouped[:])
 
-        def product1(i, a):
+        def quantize_w1(a, t0, t1, into):
+            for t in range(t0, t1):
+                codes[a, t] = into[:, 128 * (t - t0) : 128 * (t - t0 + 1)]
+            nc.vector.quantize_mx(
+                out=into[:, 0 : 128 * (t1 - t0)].bitcast(E4M3),
+                scales=w1s[:, H * a + 128 * t0 : H * a + 128 * t1],
+                in_=grouped[a][:, 512 * t0 : 512 * t1],
+            )
+
+        def product1(i, a, quarters=(0, 1, 2, 3)):
             if a == 0:
-                bank = i if i < BANKS else RING + i % (BANKS - RING)
+                bank = EARLY.index(i) if i in EARLY else RING + i % 2 + (2 if i in (12, 13) else 0)
                 acc[i] = psum.tile([P, 4, JT], F32, name="bank%d" % bank)
             s, c = divmod(i, SL // JT)
-            for t in range(4):
+            for t in quarters:
                 nc.tensor.matmul_mx(
                     out=acc[i][:, t, :],
-                    lhsT=w1c[a][:, 128 * t : 128 * t + 128].bitcast(E4M3),
+                    lhsT=codes[a, t].bitcast(E4M3),
                     lhsT_scale=w1s[:, H * a + 128 * t : H * a + 128 * t + 128],
                     rhs=words[a, s][:, JT * c : JT * c + JT].bitcast(E4M3),
                     rhs_scale=gsc[4 * a : P, JT * i : JT * i + JT],
@@ -117,10 +131,17 @@ def tile_list_tabmlp_tm_none_kernel(tc, tab, w1, w2_words, w2_scales, offs, out)
         def relu(i):
             if i in hidden or i >= TILES:
                 return
-            hidden[i] = keep.tile([P, 4 * JT], BF16, name="hidden%d" % i, align_bytes=64)
+            if i == 4:
+                held = keep.tile([P, 8 * JT], BF16, name="hc0", align_bytes=64)
+                hidden[4] = held[:, 0 : 4 * JT]
+                pending[5] = held[:, 4 * JT : 8 * JT]
+            elif i == 5:
+                hidden[5] = pending[5]
+            else:
+                hidden[i] = keep.tile([P, 4 * JT], BF16, name="hidden%d" % i, align_bytes=64)
             dst = hidden[i][:].rearrange("p (j t) -> p j t", t=4)
             src = acc[i][:].rearrange("p t j -> p j t")
-            if i in (3, 6, 9, 12):
+            if i in (3, 5, 9, 12):
                 nc.vector.tensor_scalar_max(dst, src, 0.0)
             else:
                 nc.scalar.activation(dst, src, RELU)
@@ -146,28 +167,57 @@ def tile_list_tabmlp_tm_none_kernel(tc, tab, w1, w2_words, w2_scales, offs, out)
                     start=True,
                     stop=True,
                 )
-                if (n == 0 and i not in ()) or i in (1, 5):
+                if n == (1 if i == TILES - 2 else 0) or i in (3, 5, 7):
                     nc.scalar.copy(out=ot[:, 512 * n : 512 * n + 512], in_=res[:])
                 else:
                     nc.vector.tensor_copy(ot[:, 512 * n : 512 * n + 512], res[:])
-                if i in (0, 15):
+                if i in (0,):
                     nc.sync.dma_start(out[JT * i : JT * i + JT, 512 * n : 512 * n + 512], ot[:, 512 * n : 512 * n + 512])
-            if i not in (0, 15):
+            if i not in (0,):
                 nc.sync.dma_start(out[JT * i : JT * i + JT, :], ot[:])
 
-        def gather_late(s, slot):
-            gather_words(LAST, s, s + 1, keep.tile([P, SL], U32, name=slot, align_bytes=64)[:])
+        def last_product2(i):
+            ot = ring.tile([P, M], F32, name="ot", align_bytes=64)
+            for n in range(4):
+                res = psum.tile([P, 256], F32, name="bank%d" % (2, 3, 6, 7)[n])
+                nc.tensor.matmul_mx(
+                    out=res[:],
+                    lhsT=hc[i][:].bitcast(E4M3),
+                    lhsT_scale=hs[:, JT * i : JT * i + JT],
+                    rhs=w2c[:, 512 * n : 512 * n + 512].bitcast(E2M1),
+                    rhs_scale=w2s[:, 256 * n : 256 * n + 256],
+                    start=True,
+                    stop=True,
+                )
+                if n % 2 == 0:
+                    nc.scalar.copy(out=ot[:, 256 * n : 256 * n + 256], in_=res[:])
+                else:
+                    nc.vector.tensor_copy(ot[:, 256 * n : 256 * n + 256], res[:])
+                if n > 0:
+                    c0 = 256 * n if n > 1 else 0
+                    nc.sync.dma_start(out[JT * i : JT * i + JT, c0 : 256 * n + 256], ot[:, c0 : 256 * n + 256])
+
+        def gather_late(s, slot, a=LAST):
+            gather_words(a, s, s + 1, keep.tile([P, SL], U32, name=slot, align_bytes=64)[:])
 
         gather_words(0, 2, 4, first[:, 2 * SL : 4 * SL])
-        quantize_w1(0)
-        for i in range(BANKS):
+        round_w1(0)
+        quantize_w1(0, 0, 4, w1c[0])
+        for i in EARLY:
             product1(i, 0)
-        gather_words(1, 0, 3, second[:])
-        quantize_w1(1)
-        gather_words(1, 3, 4, keep.tile([P, SL], U32, name="raw1", align_bytes=64)[:])
-        for i in range(BANKS):
-            product1(i, 1)
-        quantize_w1(LAST)
+        round_w1(1)
+        quantize_w1(1, 0, 2, w1c[1])
+        gather_words(1, 0, 2, second[:, 0 : 2 * SL])
+        for i in EARLY[:6]:
+            product1(i, 1, (0, 1))
+        gather_words(1, 2, 3, second[:, 2 * SL : 3 * SL])
+        for i in EARLY[6:]:
+            product1(i, 1, (0, 1))
+        round_w1(LAST)
+        quantize_w1(1, 2, 4, keep.tile([P, H // 2], U32, name="raw%d" % LAST, align_bytes=64))
+        for i in EARLY:
+            product1(i, 1, (2, 3))
+        quantize_w1(LAST, 0, 4, w1c[LAST])
 
         gather_words(LAST, 0, 1, front[:, 0:SL])
         for i in range(4):
@@ -176,23 +226,33 @@ def tile_list_tabmlp_tm_none_kernel(tc, tab, w1, w2_words, w2_scales, offs, out)
         relu(0)
         quantize_h(0)
         relu(1)
-        units = [(i, a) for i in range(BANKS, TILES) for a in range(PASSES)]
+        relu(2)
+        relu(3)
+        quantize_h(1)
+        product1(4, LAST)
+        product1(5, LAST)
+        units = [(i, a) for i in LATE for a in range(PASSES)]
+        units[8:8] = [(8, LAST), (9, LAST)]
         for i in range(TILES):
-            product2(i)
-            if i == 0:
+            if i == TILES - 1:
+                last_product2(i)
+            else:
+                product2(i)
+            if i in (0, 1):
+                relu(i + 4)
+            if i + 2 in hidden:
+                quantize_h(i + 2)
+            if i == 2:
                 gather_late(2, "hc%d" % i)
-            if i == 4:
+            if i == 6:
                 gather_late(3, "hc%d" % i)
-            if i < 2:
-                relu(2 * i + 2)
-                product1(2 * i + 4, LAST)
-                product1(2 * i + 5, LAST)
-                relu(3)
-            relu(i + 1)
-            quantize_h(i + 1)
-            for u, a in units[max(0, 9 * (i - 2) // 4) : max(0, 9 * (i - 1) // 4)]:
-                if a == 0:
-                    relu(u - (BANKS - RING))
+            if i == 4:
+                gather_late(3, "hc%d" % i, 1)
+            for u, a in units[max(0, 2 * (i - 1)) : 2 * i]:
                 product1(u, a)
-                if a == LAST and u >= 12:
+                if a == LAST:
                     relu(u)
+            if i + 1 in hidden:
+                quantize_h(i + 1)
+            if i == TILES - 3:
+                quantize_h(i + 2)

@@ -73,7 +73,7 @@ def tile_list_tabmlp_tm_none_kernel(tc, tab, w1, w2_words, w2_scales, offs, out)
             load_table(0)
             load_w1(0)
             for q in range(4):
-                nc.sync.dma_start(
+                (nc.sync if q < 2 else nc.gpsimd).dma_start(
                     planes[32 * q : 32 * q + 4 * PASSES, :].bitcast(I32),
                     tab[:, 512 * T + 4 * T * q : 512 * T + 4 * T * (q + 1)].rearrange("a (r t) -> a r t", r=4).bitcast(I32),
                 )

@@ -19,20 +19,28 @@ COPY = mybir.ActivationFunctionType.Copy
 P = 128
 PASSES = K // 512
 LAST = PASSES - 1
+QUARTERS = 4
 SL = 512
 JT = 128
 TILES = S // JT
-BANKS = 8
+HALF = M // 2
 RING = 4
+RESULT_BUFS = 10
+
 EARLY = (0, 1, 2, 3, 4, 5, 8, 9)
 LATE = (6, 7, 10, 11, 12, 13, 14, 15)
+AFTER_8_AND_9 = (12, 13)
+SCALE_LOADS_ON_SYNC = 1
+DEFERRED = {1: (LAST, 2), 3: (1, 3), 5: (LAST, 3)}
+VECTOR_RELUS = (3, 5, 9, 12)
+PER_STEP = 2
 
 
 def tile_list_tabmlp_tm_none_kernel(tc, tab, w1, w2_words, w2_scales, offs, out):
     nc = tc.nc
     with ExitStack() as ctx:
         keep = ctx.enter_context(tc.tile_pool(name="keep", bufs=1))
-        ring = ctx.enter_context(tc.tile_pool(name="ring", bufs=10))
+        ring = ctx.enter_context(tc.tile_pool(name="ring", bufs=RESULT_BUFS))
         psum = ctx.enter_context(tc.psum_pool(name="psum", bufs=1))
 
         lst = keep.tile([P, S // 16], U16, name="lst")
@@ -46,11 +54,12 @@ def tile_list_tabmlp_tm_none_kernel(tc, tab, w1, w2_words, w2_scales, offs, out)
         w1c = [keep.tile([P, H], U32, name="w1c%d" % a, align_bytes=64) for a in range(PASSES)]
         hs = keep.tile([P, S], U8, name="hs", align_bytes=64)
         first = keep.tile([P, S], U32, name="first", align_bytes=64)
-        hc = {}
         words = {}
+        grouped = {}
+        codes = {}
         acc = {}
         hidden = {}
-        pending = {}
+        hc = {}
 
         def load_table(a):
             nc.sync.dma_start(table[a][:], tab[a, 0 : 512 * T].rearrange("(p w) -> p w", p=P).bitcast(I32))
@@ -58,13 +67,11 @@ def tile_list_tabmlp_tm_none_kernel(tc, tab, w1, w2_words, w2_scales, offs, out)
         def load_w1(a):
             nc.sync.dma_start(raw[a][:], w1[512 * a : 512 * a + 512, :].rearrange("(p j) c -> p j c", j=4))
 
-        def entries(s0, s1):
-            return lst[:, SL // 16 * s0 : SL // 16 * s1]
-
         def gather_words(a, s0, s1, into):
             for s in range(s0, s1):
                 words[a, s] = into[:, SL * (s - s0) : SL * (s - s0 + 1)]
-            nc.vector.tensor_copy(into, table[a][:].bitcast(U32).indirect(entries(s0, s1)))
+            offsets = lst[:, SL // 16 * s0 : SL // 16 * s1]
+            nc.vector.tensor_copy(into, table[a][:].bitcast(U32).indirect(offsets))
 
         with tc.tile_pool(name="rows", bufs=1) as rows:
             planes = rows.tile([P, T], U8, name="planes", align_bytes=64)
@@ -73,14 +80,15 @@ def tile_list_tabmlp_tm_none_kernel(tc, tab, w1, w2_words, w2_scales, offs, out)
             load_table(0)
             load_w1(0)
             for q in range(4):
-                (nc.sync if q < 2 else nc.gpsimd).dma_start(
+                queue = nc.sync if q < SCALE_LOADS_ON_SYNC else nc.gpsimd
+                queue.dma_start(
                     planes[32 * q : 32 * q + 4 * PASSES, :].bitcast(I32),
                     tab[:, 512 * T + 4 * T * q : 512 * T + 4 * T * (q + 1)].rearrange("a (r t) -> a r t", r=4).bitcast(I32),
                 )
             load_w1(1)
             load_table(1)
-            load_w1(2)
-            load_table(2)
+            load_w1(LAST)
+            load_table(LAST)
             nc.sync.dma_start(w2c[:].bitcast(I32), w2_words[0].bitcast(I32))
             for q in range(4):
                 nc.sync.dma_start(w2s[32 * q : 32 * q + 4, :].bitcast(I32), w2_scales[0, 4 * q : 4 * q + 4, :].bitcast(I32))
@@ -92,167 +100,137 @@ def tile_list_tabmlp_tm_none_kernel(tc, tab, w1, w2_words, w2_scales, offs, out)
         second = later.tile([P, 3 * SL], U32, name="second", align_bytes=64)
         front = later.tile([P, 2 * SL], U32, name="front", align_bytes=64)
 
-        grouped = {}
-        codes = {}
-
         def round_w1(a):
             grouped[a] = keep.tile([P, 4 * H], BF16, name="grouped%d" % a, align_bytes=64)
             nc.scalar.activation(
-                grouped[a][:].rearrange("p (t m j) -> p m t j", t=4, j=4),
-                raw[a][:].rearrange("p j (m t) -> p m t j", t=4),
+                grouped[a][:].rearrange("p (t m j) -> p m t j", t=QUARTERS, j=4),
+                raw[a][:].rearrange("p j (m t) -> p m t j", t=QUARTERS),
                 COPY,
             )
 
         def quantize_w1(a, t0, t1, into):
             for t in range(t0, t1):
-                codes[a, t] = into[:, 128 * (t - t0) : 128 * (t - t0 + 1)]
+                codes[a, t] = into[:, P * (t - t0) : P * (t - t0 + 1)]
             nc.vector.quantize_mx(
-                out=into[:, 0 : 128 * (t1 - t0)].bitcast(E4M3),
-                scales=w1s[:, H * a + 128 * t0 : H * a + 128 * t1],
-                in_=grouped[a][:, 512 * t0 : 512 * t1],
+                out=into[:, 0 : P * (t1 - t0)].bitcast(E4M3),
+                scales=w1s[:, H * a + P * t0 : H * a + P * t1],
+                in_=grouped[a][:, 4 * P * t0 : 4 * P * t1],
             )
 
-        def product1(i, a, quarters=(0, 1, 2, 3)):
+        def product1(i, a, t0=0, t1=QUARTERS):
             if a == 0:
-                bank = EARLY.index(i) if i in EARLY else RING + i % 2 + (2 if i in (12, 13) else 0)
-                acc[i] = psum.tile([P, 4, JT], F32, name="bank%d" % bank)
+                bank = EARLY.index(i) if i in EARLY else RING + i % 2 + (2 if i in AFTER_8_AND_9 else 0)
+                acc[i] = psum.tile([P, QUARTERS, JT], F32, name="bank%d" % bank)
             s, c = divmod(i, SL // JT)
-            for t in quarters:
+            for t in range(t0, t1):
                 nc.tensor.matmul_mx(
                     out=acc[i][:, t, :],
                     lhsT=codes[a, t].bitcast(E4M3),
-                    lhsT_scale=w1s[:, H * a + 128 * t : H * a + 128 * t + 128],
+                    lhsT_scale=w1s[:, H * a + P * t : H * a + P * t + P],
                     rhs=words[a, s][:, JT * c : JT * c + JT].bitcast(E4M3),
                     rhs_scale=gsc[4 * a : P, JT * i : JT * i + JT],
                     start=(a == 0 and t == 0),
-                    stop=(a == LAST and t == 3),
+                    stop=(a == LAST and t == QUARTERS - 1),
                 )
 
-        def relu(i):
-            if i in hidden or i >= TILES:
-                return
-            if i == 4:
-                held = keep.tile([P, 8 * JT], BF16, name="hc0", align_bytes=64)
-                hidden[4] = held[:, 0 : 4 * JT]
-                pending[5] = held[:, 4 * JT : 8 * JT]
-            elif i == 5:
-                hidden[5] = pending[5]
-            else:
-                hidden[i] = keep.tile([P, 4 * JT], BF16, name="hidden%d" % i, align_bytes=64)
-            dst = hidden[i][:].rearrange("p (j t) -> p j t", t=4)
+        def relu(i, into=None):
+            if into is None:
+                into = keep.tile([P, QUARTERS * JT], BF16, name="hidden%d" % i, align_bytes=64)[:]
+            hidden[i] = into
+            dst = into.rearrange("p (j t) -> p j t", t=QUARTERS)
             src = acc[i][:].rearrange("p t j -> p j t")
-            if i in (3, 5, 9, 12):
+            if i in VECTOR_RELUS:
                 nc.vector.tensor_scalar_max(dst, src, 0.0)
             else:
                 nc.scalar.activation(dst, src, RELU)
 
         def quantize_h(i):
-            if i in hc or i >= TILES:
-                return
-            hc[i] = keep.tile([P, JT], U32, name="hc%d" % i, align_bytes=64)
-            nc.vector.quantize_mx(
-                out=hc[i][:].bitcast(E4M3), scales=hs[:, JT * i : JT * i + JT], in_=hidden[i][:]
+            if i in hidden and i not in hc:
+                hc[i] = keep.tile([P, JT], U32, name="hc%d" % i, align_bytes=64)
+                nc.vector.quantize_mx(out=hc[i][:].bitcast(E4M3), scales=hs[:, JT * i : JT * i + JT], in_=hidden[i])
+
+        def piece_of_out(i, ot, c0, width, bank, on_scalar):
+            res = psum.tile([P, width], F32, name="bank%d" % bank)
+            nc.tensor.matmul_mx(
+                out=res[:],
+                lhsT=hc[i][:].bitcast(E4M3),
+                lhsT_scale=hs[:, JT * i : JT * i + JT],
+                rhs=w2c[:, 2 * c0 : 2 * (c0 + width)].bitcast(E2M1),
+                rhs_scale=w2s[:, c0 : c0 + width],
+                start=True,
+                stop=True,
             )
+            if on_scalar:
+                nc.scalar.copy(out=ot[:, c0 : c0 + width], in_=res[:])
+            else:
+                nc.vector.tensor_copy(ot[:, c0 : c0 + width], res[:])
+
+        def store(i, ot, c0, c1):
+            nc.sync.dma_start(out[JT * i : JT * i + JT, c0:c1], ot[:, c0:c1])
 
         def product2(i):
             ot = ring.tile([P, M], F32, name="ot", align_bytes=64)
+            if i == TILES - 1:
+                width = HALF // 2
+                for n, bank in enumerate((2, 3, 6, 7)):
+                    piece_of_out(i, ot, width * n, width, bank, n % 2 == 0)
+                    if n > 0:
+                        store(i, ot, width * n if n > 1 else 0, width * (n + 1))
+                return
+            scalar_half = 1 if i == TILES - 2 else 0
             for n in range(2):
-                res = psum.tile([P, 512], F32, name="bank%d" % ((2 * i + n) % RING))
-                nc.tensor.matmul_mx(
-                    out=res[:],
-                    lhsT=hc[i][:].bitcast(E4M3),
-                    lhsT_scale=hs[:, JT * i : JT * i + JT],
-                    rhs=w2c[:, 1024 * n : 1024 * n + 1024].bitcast(E2M1),
-                    rhs_scale=w2s[:, 512 * n : 512 * n + 512],
-                    start=True,
-                    stop=True,
-                )
-                if n == (1 if i == TILES - 2 else 0) or i in (3, 5, 7):
-                    nc.scalar.copy(out=ot[:, 512 * n : 512 * n + 512], in_=res[:])
-                else:
-                    nc.vector.tensor_copy(ot[:, 512 * n : 512 * n + 512], res[:])
-                if i in (0,):
-                    nc.sync.dma_start(out[JT * i : JT * i + JT, 512 * n : 512 * n + 512], ot[:, 512 * n : 512 * n + 512])
-            if i not in (0,):
-                nc.sync.dma_start(out[JT * i : JT * i + JT, :], ot[:])
-
-        def last_product2(i):
-            ot = ring.tile([P, M], F32, name="ot", align_bytes=64)
-            for n in range(4):
-                res = psum.tile([P, 256], F32, name="bank%d" % (2, 3, 6, 7)[n])
-                nc.tensor.matmul_mx(
-                    out=res[:],
-                    lhsT=hc[i][:].bitcast(E4M3),
-                    lhsT_scale=hs[:, JT * i : JT * i + JT],
-                    rhs=w2c[:, 512 * n : 512 * n + 512].bitcast(E2M1),
-                    rhs_scale=w2s[:, 256 * n : 256 * n + 256],
-                    start=True,
-                    stop=True,
-                )
-                if n % 2 == 0:
-                    nc.scalar.copy(out=ot[:, 256 * n : 256 * n + 256], in_=res[:])
-                else:
-                    nc.vector.tensor_copy(ot[:, 256 * n : 256 * n + 256], res[:])
-                if n > 0:
-                    c0 = 256 * n if n > 1 else 0
-                    nc.sync.dma_start(out[JT * i : JT * i + JT, c0 : 256 * n + 256], ot[:, c0 : 256 * n + 256])
-
-        def gather_late(s, slot, a=LAST):
-            gather_words(a, s, s + 1, keep.tile([P, SL], U32, name=slot, align_bytes=64)[:])
+                piece_of_out(i, ot, HALF * n, HALF, (2 * i + n) % RING, n == scalar_half or i - 1 in DEFERRED)
+                if i == 0:
+                    store(i, ot, HALF * n, HALF * (n + 1))
+            if i > 0:
+                store(i, ot, 0, M)
 
         gather_words(0, 2, 4, first[:, 2 * SL : 4 * SL])
         round_w1(0)
-        quantize_w1(0, 0, 4, w1c[0])
+        quantize_w1(0, 0, QUARTERS, w1c[0])
         for i in EARLY:
             product1(i, 0)
         round_w1(1)
         quantize_w1(1, 0, 2, w1c[1])
         gather_words(1, 0, 2, second[:, 0 : 2 * SL])
-        for i in EARLY[:6]:
-            product1(i, 1, (0, 1))
-        gather_words(1, 2, 3, second[:, 2 * SL : 3 * SL])
-        for i in EARLY[6:]:
-            product1(i, 1, (0, 1))
-        round_w1(LAST)
-        quantize_w1(1, 2, 4, keep.tile([P, H // 2], U32, name="raw%d" % LAST, align_bytes=64))
         for i in EARLY:
-            product1(i, 1, (2, 3))
-        quantize_w1(LAST, 0, 4, w1c[LAST])
+            if i == 2 * SL // JT:
+                gather_words(1, 2, 3, second[:, 2 * SL : 3 * SL])
+            product1(i, 1, 0, 2)
+        round_w1(LAST)
+        quantize_w1(1, 2, QUARTERS, keep.tile([P, H // 2], U32, name="raw%d" % LAST, align_bytes=64))
+        for i in EARLY:
+            product1(i, 1, 2, QUARTERS)
+        quantize_w1(LAST, 0, QUARTERS, w1c[LAST])
 
         gather_words(LAST, 0, 1, front[:, 0:SL])
-        for i in range(4):
+        for i in range(RING):
             product1(i, LAST)
         gather_words(LAST, 1, 2, front[:, SL : 2 * SL])
         relu(0)
         quantize_h(0)
-        relu(1)
-        relu(2)
-        relu(3)
+        for i in range(1, RING):
+            relu(i)
         quantize_h(1)
         product1(4, LAST)
         product1(5, LAST)
-        units = [(i, a) for i in LATE for a in range(PASSES)]
-        units[8:8] = [(8, LAST), (9, LAST)]
+
+        left = [(i, a) for i in LATE for a in range(PASSES)]
+        left[2 * PASSES : 2 * PASSES] = [(8, LAST), (9, LAST)]
         for i in range(TILES):
-            if i == TILES - 1:
-                last_product2(i)
-            else:
-                product2(i)
-            if i in (0, 1):
-                relu(i + 4)
-            if i + 2 in hidden:
-                quantize_h(i + 2)
-            if i == 2:
-                gather_late(2, "hc%d" % i)
-            if i == 6:
-                gather_late(3, "hc%d" % i)
-            if i == 4:
-                gather_late(3, "hc%d" % i, 1)
-            for u, a in units[max(0, 2 * (i - 1)) : 2 * i]:
+            product2(i)
+            if i == 0:
+                held = keep.tile([P, 2 * QUARTERS * JT], BF16, name="hc0", align_bytes=64)
+            if i < 2:
+                relu(RING + i, held[:, QUARTERS * JT * i : QUARTERS * JT * (i + 1)])
+            quantize_h(i + 2)
+            if i in DEFERRED:
+                a, s = DEFERRED[i]
+                gather_words(a, s, s + 1, keep.tile([P, SL], U32, name="hc%d" % i, align_bytes=64)[:])
+            for u, a in left[max(0, PER_STEP * (i - 1)) : PER_STEP * i]:
                 product1(u, a)
                 if a == LAST:
                     relu(u)
-            if i + 1 in hidden:
-                quantize_h(i + 1)
+            quantize_h(i + 1)
             if i == TILES - 3:
                 quantize_h(i + 2)

@@ -27,13 +27,18 @@ HALF = M // 2
 RING = 4
 RESULT_BUFS = 10
 
-EARLY = (0, 1, 2, 3, 4, 5, 8, 9)
-LATE = (6, 7, 10, 11, 12, 13, 14, 15)
-AFTER_8_AND_9 = (12, 13)
+EARLY = tuple(range(8))
+LATE = tuple(i for i in range(TILES) if i not in EARLY)
 SCALE_LOADS_ON_SYNC = 1
-DEFERRED = {1: (LAST, 2), 3: (1, 3), 5: (LAST, 3)}
-VECTOR_RELUS = (3, 5, 9, 12)
-PER_STEP = 2
+FRONT = 6
+DEFERRED = {1: (2, 6), 2: (2, 8), 4: (2, 10), 6: (2, 12), 8: (1, 14), 10: (2, 14)}
+VECTOR_RELUS = (3,)
+AHEAD = 6
+LAG = 4
+FIRST = ((0, 512), (512, 1024))
+FIRST_STORES = ((0, 512), (512, 1024))
+LAST_STORES = ((0, 512), (512, 1024))
+PER_STEP = lambda i: 2 if i else 0
 
 
 def tile_list_tabmlp_tm_none_kernel(tc, tab, w1, w2_words, w2_scales, offs, out):
@@ -52,7 +57,6 @@ def tile_list_tabmlp_tm_none_kernel(tc, tab, w1, w2_words, w2_scales, offs, out)
         w2s = keep.tile([P, M], U8, name="w2s", align_bytes=64)
         gsc = keep.tile([P, S], U8, name="gsc", align_bytes=64)
         w1c = [keep.tile([P, H], U32, name="w1c%d" % a, align_bytes=64) for a in range(PASSES)]
-        hs = keep.tile([P, S], U8, name="hs", align_bytes=64)
         first = keep.tile([P, S], U32, name="first", align_bytes=64)
         words = {}
         grouped = {}
@@ -60,6 +64,7 @@ def tile_list_tabmlp_tm_none_kernel(tc, tab, w1, w2_words, w2_scales, offs, out)
         acc = {}
         hidden = {}
         hc = {}
+        hs = {}
 
         def load_table(a):
             nc.sync.dma_start(table[a][:], tab[a, 0 : 512 * T].rearrange("(p w) -> p w", p=P).bitcast(I32))
@@ -67,10 +72,10 @@ def tile_list_tabmlp_tm_none_kernel(tc, tab, w1, w2_words, w2_scales, offs, out)
         def load_w1(a):
             nc.sync.dma_start(raw[a][:], w1[512 * a : 512 * a + 512, :].rearrange("(p j) c -> p j c", j=4))
 
-        def gather_words(a, s0, s1, into):
-            for s in range(s0, s1):
-                words[a, s] = into[:, SL * (s - s0) : SL * (s - s0 + 1)]
-            offsets = lst[:, SL // 16 * s0 : SL // 16 * s1]
+        def gather_words(a, i0, i1, into):
+            for i in range(i0, i1):
+                words[a, i] = into[:, JT * (i - i0) : JT * (i - i0 + 1)]
+            offsets = lst[:, JT // 16 * i0 : JT // 16 * i1]
             nc.vector.tensor_copy(into, table[a][:].bitcast(U32).indirect(offsets))
 
         with tc.tile_pool(name="rows", bufs=1) as rows:
@@ -92,13 +97,14 @@ def tile_list_tabmlp_tm_none_kernel(tc, tab, w1, w2_words, w2_scales, offs, out)
             nc.sync.dma_start(w2c[:].bitcast(I32), w2_words[0].bitcast(I32))
             for q in range(4):
                 nc.sync.dma_start(w2s[32 * q : 32 * q + 4, :].bitcast(I32), w2_scales[0, 4 * q : 4 * q + 4, :].bitcast(I32))
-            gather_words(0, 0, 2, first[:, 0 : 2 * SL])
+            gather_words(0, 0, TILES, first[:])
             nc.vector.tensor_copy(gsc[:], planes[:].indirect(lst[:]))
 
         later = ctx.enter_context(tc.tile_pool(name="later", bufs=1))
         w1s = later.tile([P, PASSES * H], U8, name="w1s", align_bytes=64)
-        second = later.tile([P, 3 * SL], U32, name="second", align_bytes=64)
-        front = later.tile([P, 2 * SL], U32, name="front", align_bytes=64)
+        second = later.tile([P, 14 * JT], U32, name="second", align_bytes=64)
+        front = later.tile([P, FRONT * JT], U32, name="front", align_bytes=64)
+        turn = [0]
 
         def round_w1(a):
             grouped[a] = keep.tile([P, 4 * H], BF16, name="grouped%d" % a, align_bytes=64)
@@ -119,23 +125,22 @@ def tile_list_tabmlp_tm_none_kernel(tc, tab, w1, w2_words, w2_scales, offs, out)
 
         def product1(i, a, t0=0, t1=QUARTERS):
             if a == 0:
-                bank = EARLY.index(i) if i in EARLY else RING + i % 2 + (2 if i in AFTER_8_AND_9 else 0)
+                bank = EARLY.index(i) if i in EARLY else RING + LATE.index(i) % RING
                 acc[i] = psum.tile([P, QUARTERS, JT], F32, name="bank%d" % bank)
-            s, c = divmod(i, SL // JT)
             for t in range(t0, t1):
                 nc.tensor.matmul_mx(
                     out=acc[i][:, t, :],
                     lhsT=codes[a, t].bitcast(E4M3),
                     lhsT_scale=w1s[:, H * a + P * t : H * a + P * t + P],
-                    rhs=words[a, s][:, JT * c : JT * c + JT].bitcast(E4M3),
+                    rhs=words[a, i].bitcast(E4M3),
                     rhs_scale=gsc[4 * a : P, JT * i : JT * i + JT],
                     start=(a == 0 and t == 0),
                     stop=(a == LAST and t == QUARTERS - 1),
                 )
 
-        def relu(i, into=None):
-            if into is None:
-                into = keep.tile([P, QUARTERS * JT], BF16, name="hidden%d" % i, align_bytes=64)[:]
+        def relu(i):
+            name = "hc%d" % (i - LAG) if i >= LAG else "hidden%d" % i
+            into = keep.tile([P, QUARTERS * JT], BF16, name=name, align_bytes=64)[:]
             hidden[i] = into
             dst = into.rearrange("p (j t) -> p j t", t=QUARTERS)
             src = acc[i][:].rearrange("p t j -> p j t")
@@ -147,14 +152,15 @@ def tile_list_tabmlp_tm_none_kernel(tc, tab, w1, w2_words, w2_scales, offs, out)
         def quantize_h(i):
             if i in hidden and i not in hc:
                 hc[i] = keep.tile([P, JT], U32, name="hc%d" % i, align_bytes=64)
-                nc.vector.quantize_mx(out=hc[i][:].bitcast(E4M3), scales=hs[:, JT * i : JT * i + JT], in_=hidden[i])
+                hs[i] = keep.tile([P, JT], U8, name="hs%d" % i, align_bytes=64)
+                nc.vector.quantize_mx(out=hc[i][:].bitcast(E4M3), scales=hs[i][:], in_=hidden[i])
 
         def piece_of_out(i, ot, c0, width, bank, on_scalar):
             res = psum.tile([P, width], F32, name="bank%d" % bank)
             nc.tensor.matmul_mx(
                 out=res[:],
                 lhsT=hc[i][:].bitcast(E4M3),
-                lhsT_scale=hs[:, JT * i : JT * i + JT],
+                lhsT_scale=hs[i][:],
                 rhs=w2c[:, 2 * c0 : 2 * (c0 + width)].bitcast(E2M1),
                 rhs_scale=w2s[:, c0 : c0 + width],
                 start=True,
@@ -165,37 +171,32 @@ def tile_list_tabmlp_tm_none_kernel(tc, tab, w1, w2_words, w2_scales, offs, out)
             else:
                 nc.vector.tensor_copy(ot[:, c0 : c0 + width], res[:])
 
-        def store(i, ot, c0, c1):
-            nc.sync.dma_start(out[JT * i : JT * i + JT, c0:c1], ot[:, c0:c1])
-
         def product2(i):
             ot = ring.tile([P, M], F32, name="ot", align_bytes=64)
+            stores = FIRST_STORES if i == 0 else LAST_STORES if i == TILES - 1 else ((0, M),)
             if i == TILES - 1:
-                width = HALF // 2
-                for n, bank in enumerate((2, 3, 6, 7)):
-                    piece_of_out(i, ot, width * n, width, bank, n % 2 == 0)
-                    if n > 0:
-                        store(i, ot, width * n if n > 1 else 0, width * (n + 1))
-                return
-            scalar_half = 1 if i == TILES - 2 else 0
-            for n in range(2):
-                piece_of_out(i, ot, HALF * n, HALF, (2 * i + n) % RING, n == scalar_half or i - 1 in DEFERRED)
-                if i == 0:
-                    store(i, ot, HALF * n, HALF * (n + 1))
-            if i > 0:
-                store(i, ot, 0, M)
+                pieces = [(c, c + HALF // 2) for c in range(0, M, HALF // 2)]
+                banks = (turn[0] % RING, (turn[0] + 1) % RING, 4, 5)
+            else:
+                pieces = FIRST if i == 0 else ((0, HALF), (HALF, M))
+                banks = [(turn[0] + n) % RING for n in range(len(pieces))]
+                turn[0] = turn[0] + len(pieces)
+            for n, (c0, c1) in enumerate(pieces):
+                on_scalar = (n % 2 == (1 if i == TILES - 2 else 0)) or (False)
+                piece_of_out(i, ot, c0, c1 - c0, banks[n], on_scalar)
+                for s0, s1 in stores:
+                    if s1 == c1:
+                        nc.sync.dma_start(out[JT * i : JT * i + JT, s0:s1], ot[:, s0:s1])
 
-        gather_words(0, 2, 4, first[:, 2 * SL : 4 * SL])
         round_w1(0)
         quantize_w1(0, 0, QUARTERS, w1c[0])
         for i in EARLY:
             product1(i, 0)
         round_w1(1)
         quantize_w1(1, 0, 2, w1c[1])
-        gather_words(1, 0, 2, second[:, 0 : 2 * SL])
+        gather_words(1, 0, 8, second[:, 0 : 2 * SL])
+        gather_words(1, 8, 14, second[:, 2 * SL : 14 * JT])
         for i in EARLY:
-            if i == 2 * SL // JT:
-                gather_words(1, 2, 3, second[:, 2 * SL : 3 * SL])
             product1(i, 1, 0, 2)
         round_w1(LAST)
         quantize_w1(1, 2, QUARTERS, keep.tile([P, H // 2], U32, name="raw%d" % LAST, align_bytes=64))
@@ -203,34 +204,38 @@ def tile_list_tabmlp_tm_none_kernel(tc, tab, w1, w2_words, w2_scales, offs, out)
             product1(i, 1, 2, QUARTERS)
         quantize_w1(LAST, 0, QUARTERS, w1c[LAST])
 
-        gather_words(LAST, 0, 1, front[:, 0:SL])
+        for i in range(0, FRONT, 2):
+            gather_words(LAST, i, i + 2, front[:, JT * i : JT * (i + 2)])
         for i in range(RING):
             product1(i, LAST)
-        gather_words(LAST, 1, 2, front[:, SL : 2 * SL])
         relu(0)
         quantize_h(0)
-        for i in range(1, RING):
-            relu(i)
+        relu(1)
         quantize_h(1)
-        product1(4, LAST)
-        product1(5, LAST)
 
-        left = [(i, a) for i in LATE for a in range(PASSES)]
-        left[2 * PASSES : 2 * PASSES] = [(8, LAST), (9, LAST)]
+        for i in range(2, RING):
+            relu(i)
+        for i in EARLY[RING:AHEAD]:
+            product1(i, LAST)
+
+        left = [(8, 0), (8, 1)] + [(i, LAST) for i in EARLY[AHEAD:]] + [(i, a) for i in LATE for a in range(PASSES)][2:]
+        waiting = list(EARLY[RING:AHEAD])
+        done = 0
         for i in range(TILES):
             product2(i)
-            if i == 0:
-                held = keep.tile([P, 2 * QUARTERS * JT], BF16, name="hc0", align_bytes=64)
-            if i < 2:
-                relu(RING + i, held[:, QUARTERS * JT * i : QUARTERS * JT * (i + 1)])
-            quantize_h(i + 2)
+            quantize_h(i + 1)
             if i in DEFERRED:
-                a, s = DEFERRED[i]
-                gather_words(a, s, s + 1, keep.tile([P, SL], U32, name="hc%d" % i, align_bytes=64)[:])
-            for u, a in left[max(0, PER_STEP * (i - 1)) : PER_STEP * i]:
+                a, u = DEFERRED[i]
+                gather_words(a, u, u + 2, keep.tile([P, 2 * JT], U32, name="hs%d" % i, align_bytes=64)[:])
+            for u, a in left[done : done + PER_STEP(i)]:
                 product1(u, a)
                 if a == LAST:
+                    waiting.append(u)
+            done += PER_STEP(i)
+            for u in list(waiting):
+                if u <= i + LAG:
                     relu(u)
-            quantize_h(i + 1)
-            if i == TILES - 3:
-                quantize_h(i + 2)
+                    waiting.remove(u)
+            for u in range(i + 1, i + 1 + 1):
+                quantize_h(u)
+        assert done >= len(left)

@@ -20,25 +20,20 @@ P = 128
 PASSES = K // 512
 LAST = PASSES - 1
 QUARTERS = 4
-SL = 512
 JT = 128
 TILES = S // JT
 HALF = M // 2
+BANKS = 8
 RING = 4
 RESULT_BUFS = 10
+PAIR = 2
 
-EARLY = tuple(range(8))
-LATE = tuple(i for i in range(TILES) if i not in EARLY)
 SCALE_LOADS_ON_SYNC = 1
+GATHERED_EARLY = TILES - PAIR
 FRONT = 6
-DEFERRED = {1: (2, 6), 2: (2, 8), 4: (2, 10), 6: (2, 12), 8: (1, 14), 10: (2, 14)}
-VECTOR_RELUS = (3,)
-AHEAD = 6
-LAG = 4
-FIRST = ((0, 512), (512, 1024))
-FIRST_STORES = ((0, 512), (512, 1024))
-LAST_STORES = ((0, 512), (512, 1024))
-PER_STEP = lambda i: 2 if i else 0
+VECTOR_RELU = RING - 1
+PER_STEP = 2
+LEAD = 2
 
 
 def tile_list_tabmlp_tm_none_kernel(tc, tab, w1, w2_words, w2_scales, offs, out):
@@ -102,9 +97,8 @@ def tile_list_tabmlp_tm_none_kernel(tc, tab, w1, w2_words, w2_scales, offs, out)
 
         later = ctx.enter_context(tc.tile_pool(name="later", bufs=1))
         w1s = later.tile([P, PASSES * H], U8, name="w1s", align_bytes=64)
-        second = later.tile([P, 14 * JT], U32, name="second", align_bytes=64)
+        second = later.tile([P, GATHERED_EARLY * JT], U32, name="second", align_bytes=64)
         front = later.tile([P, FRONT * JT], U32, name="front", align_bytes=64)
-        turn = [0]
 
         def round_w1(a):
             grouped[a] = keep.tile([P, 4 * H], BF16, name="grouped%d" % a, align_bytes=64)
@@ -125,7 +119,7 @@ def tile_list_tabmlp_tm_none_kernel(tc, tab, w1, w2_words, w2_scales, offs, out)
 
         def product1(i, a, t0=0, t1=QUARTERS):
             if a == 0:
-                bank = EARLY.index(i) if i in EARLY else RING + LATE.index(i) % RING
+                bank = i if i < BANKS else RING + i % RING
                 acc[i] = psum.tile([P, QUARTERS, JT], F32, name="bank%d" % bank)
             for t in range(t0, t1):
                 nc.tensor.matmul_mx(
@@ -139,103 +133,97 @@ def tile_list_tabmlp_tm_none_kernel(tc, tab, w1, w2_words, w2_scales, offs, out)
                 )
 
         def relu(i):
-            name = "hc%d" % (i - LAG) if i >= LAG else "hidden%d" % i
-            into = keep.tile([P, QUARTERS * JT], BF16, name=name, align_bytes=64)[:]
-            hidden[i] = into
-            dst = into.rearrange("p (j t) -> p j t", t=QUARTERS)
+            name = "hc%d" % (i - RING) if i >= RING else "hidden%d" % i
+            hidden[i] = keep.tile([P, QUARTERS * JT], BF16, name=name, align_bytes=64)
+            dst = hidden[i][:].rearrange("p (j t) -> p j t", t=QUARTERS)
             src = acc[i][:].rearrange("p t j -> p j t")
-            if i in VECTOR_RELUS:
+            if i == VECTOR_RELU:
                 nc.vector.tensor_scalar_max(dst, src, 0.0)
             else:
                 nc.scalar.activation(dst, src, RELU)
 
         def quantize_h(i):
-            if i in hidden and i not in hc:
-                hc[i] = keep.tile([P, JT], U32, name="hc%d" % i, align_bytes=64)
-                hs[i] = keep.tile([P, JT], U8, name="hs%d" % i, align_bytes=64)
-                nc.vector.quantize_mx(out=hc[i][:].bitcast(E4M3), scales=hs[i][:], in_=hidden[i])
-
-        def piece_of_out(i, ot, c0, width, bank, on_scalar):
-            res = psum.tile([P, width], F32, name="bank%d" % bank)
-            nc.tensor.matmul_mx(
-                out=res[:],
-                lhsT=hc[i][:].bitcast(E4M3),
-                lhsT_scale=hs[i][:],
-                rhs=w2c[:, 2 * c0 : 2 * (c0 + width)].bitcast(E2M1),
-                rhs_scale=w2s[:, c0 : c0 + width],
-                start=True,
-                stop=True,
-            )
-            if on_scalar:
-                nc.scalar.copy(out=ot[:, c0 : c0 + width], in_=res[:])
-            else:
-                nc.vector.tensor_copy(ot[:, c0 : c0 + width], res[:])
+            hc[i] = keep.tile([P, JT], U32, name="hc%d" % i, align_bytes=64)
+            hs[i] = keep.tile([P, JT], U8, name="hs%d" % i, align_bytes=64)
+            nc.vector.quantize_mx(out=hc[i][:].bitcast(E4M3), scales=hs[i][:], in_=hidden[i][:])
 
         def product2(i):
             ot = ring.tile([P, M], F32, name="ot", align_bytes=64)
-            stores = FIRST_STORES if i == 0 else LAST_STORES if i == TILES - 1 else ((0, M),)
+            banks = [2 * i % RING, (2 * i + 1) % RING]
             if i == TILES - 1:
-                pieces = [(c, c + HALF // 2) for c in range(0, M, HALF // 2)]
-                banks = (turn[0] % RING, (turn[0] + 1) % RING, 4, 5)
-            else:
-                pieces = FIRST if i == 0 else ((0, HALF), (HALF, M))
-                banks = [(turn[0] + n) % RING for n in range(len(pieces))]
-                turn[0] = turn[0] + len(pieces)
-            for n, (c0, c1) in enumerate(pieces):
-                on_scalar = (n % 2 == (1 if i == TILES - 2 else 0)) or (False)
-                piece_of_out(i, ot, c0, c1 - c0, banks[n], on_scalar)
-                for s0, s1 in stores:
-                    if s1 == c1:
-                        nc.sync.dma_start(out[JT * i : JT * i + JT, s0:s1], ot[:, s0:s1])
+                banks.extend([RING, RING + 1])
+            width = M // len(banks)
+            scalar_turn = 1 if i == TILES - 2 else 0
+            stored = HALF if i in (0, TILES - 1) else M
+            for n, bank in enumerate(banks):
+                c0, c1 = width * n, width * (n + 1)
+                res = psum.tile([P, width], F32, name="bank%d" % bank)
+                nc.tensor.matmul_mx(
+                    out=res[:],
+                    lhsT=hc[i][:].bitcast(E4M3),
+                    lhsT_scale=hs[i][:],
+                    rhs=w2c[:, 2 * c0 : 2 * c1].bitcast(E2M1),
+                    rhs_scale=w2s[:, c0:c1],
+                    start=True,
+                    stop=True,
+                )
+                if n % 2 == scalar_turn:
+                    nc.scalar.copy(out=ot[:, c0:c1], in_=res[:])
+                else:
+                    nc.vector.tensor_copy(ot[:, c0:c1], res[:])
+                if c1 % stored == 0:
+                    nc.sync.dma_start(out[JT * i : JT * i + JT, c1 - stored : c1], ot[:, c1 - stored : c1])
 
         round_w1(0)
         quantize_w1(0, 0, QUARTERS, w1c[0])
-        for i in EARLY:
+        for i in range(BANKS):
             product1(i, 0)
         round_w1(1)
         quantize_w1(1, 0, 2, w1c[1])
-        gather_words(1, 0, 8, second[:, 0 : 2 * SL])
-        gather_words(1, 8, 14, second[:, 2 * SL : 14 * JT])
-        for i in EARLY:
+        gather_words(1, 0, BANKS, second[:, 0 : BANKS * JT])
+        gather_words(1, BANKS, GATHERED_EARLY, second[:, BANKS * JT : GATHERED_EARLY * JT])
+        for i in range(BANKS):
             product1(i, 1, 0, 2)
         round_w1(LAST)
         quantize_w1(1, 2, QUARTERS, keep.tile([P, H // 2], U32, name="raw%d" % LAST, align_bytes=64))
-        for i in EARLY:
+        for i in range(BANKS):
             product1(i, 1, 2, QUARTERS)
         quantize_w1(LAST, 0, QUARTERS, w1c[LAST])
 
-        for i in range(0, FRONT, 2):
-            gather_words(LAST, i, i + 2, front[:, JT * i : JT * (i + 2)])
+        for i in range(0, FRONT, PAIR):
+            gather_words(LAST, i, i + PAIR, front[:, JT * i : JT * (i + PAIR)])
         for i in range(RING):
             product1(i, LAST)
-        relu(0)
-        quantize_h(0)
-        relu(1)
-        quantize_h(1)
-
-        for i in range(2, RING):
+        for i in range(RING):
             relu(i)
-        for i in EARLY[RING:AHEAD]:
+            if i < 2:
+                quantize_h(i)
+        for i in range(RING, FRONT):
             product1(i, LAST)
 
-        left = [(8, 0), (8, 1)] + [(i, LAST) for i in EARLY[AHEAD:]] + [(i, a) for i in LATE for a in range(PASSES)][2:]
-        waiting = list(EARLY[RING:AHEAD])
-        done = 0
+        left = [(i, a) for i in range(BANKS, BANKS + PAIR) for a in range(LAST)]
+        left.extend((i, LAST) for i in range(FRONT, BANKS + PAIR))
+        left.extend((i, a) for i in range(BANKS + PAIR, TILES) for a in range(PASSES))
+        passes = {i: left[PER_STEP * (i - 1) : PER_STEP * i] for i in range(1, TILES)}
+        gathers = {}
+        for i in range(1, TILES):
+            for u, a in passes[i]:
+                if (a, u) not in words and u % PAIR == 0:
+                    gathers[i - LEAD] = (a, u)
+
+        summed = list(range(RING, FRONT))
         for i in range(TILES):
             product2(i)
-            quantize_h(i + 1)
-            if i in DEFERRED:
-                a, u = DEFERRED[i]
-                gather_words(a, u, u + 2, keep.tile([P, 2 * JT], U32, name="hs%d" % i, align_bytes=64)[:])
-            for u, a in left[done : done + PER_STEP(i)]:
+            if 0 < i < TILES - 1:
+                quantize_h(i + 1)
+            if i in gathers:
+                a, u = gathers[i]
+                gather_words(a, u, u + PAIR, keep.tile([P, PAIR * JT], U32, name="hs%d" % i, align_bytes=64)[:])
+            for u, a in passes.get(i, ()):
                 product1(u, a)
                 if a == LAST:
-                    waiting.append(u)
-            done += PER_STEP(i)
-            for u in list(waiting):
-                if u <= i + LAG:
+                    summed.append(u)
+            for u in list(summed):
+                if u <= i + RING:
                     relu(u)
-                    waiting.remove(u)
-            for u in range(i + 1, i + 1 + 1):
-                quantize_h(u)
-        assert done >= len(left)
+                    summed.remove(u)

@@ -154,7 +154,7 @@ def tile_list_tabmlp_tm_none_kernel(tc, tab, w1, w2_words, w2_scales, offs, out)
                 banks.extend([RING, RING + 1])
             width = M // len(banks)
             scalar_turn = 1 if i == TILES - 2 else 0
-            stored = HALF if i in (0, TILES - 1) else M
+            stored = HALF if i == 0 else M
             for n, bank in enumerate(banks):
                 c0, c1 = width * n, width * (n + 1)
                 res = psum.tile([P, width], F32, name="bank%d" % bank)

@@ -25,22 +25,19 @@ TILES = S // JT
 HALF = M // 2
 BANKS = 8
 RING = 4
-RESULT_BUFS = 10
 PAIR = 2
-
 SCALE_LOADS_ON_SYNC = 1
-GATHERED_EARLY = TILES - PAIR
+GATHERED_EARLY = 14
 FRONT = 6
-VECTOR_RELU = RING - 1
-PER_STEP = 2
 LEAD = 2
+VECTOR_RELUS = (3,7,8,9,10,11,12,13,14)
+GROUPS = [(0, 1), (1, 1), (2, 1), (3, 1), (4, 1), (5, 1), (6, 1), (7, 1), (8, 1), (9, 1), (10, 1), (11, 1), (12, 1), (13, 1), (14, 1), (15, 1)]
 
 
 def tile_list_tabmlp_tm_none_kernel(tc, tab, w1, w2_words, w2_scales, offs, out):
     nc = tc.nc
     with ExitStack() as ctx:
         keep = ctx.enter_context(tc.tile_pool(name="keep", bufs=1))
-        ring = ctx.enter_context(tc.tile_pool(name="ring", bufs=RESULT_BUFS))
         psum = ctx.enter_context(tc.psum_pool(name="psum", bufs=1))
 
         lst = keep.tile([P, S // 16], U16, name="lst")
@@ -58,6 +55,12 @@ def tile_list_tabmlp_tm_none_kernel(tc, tab, w1, w2_words, w2_scales, offs, out)
         codes = {}
         acc = {}
         hidden = {}
+        joined = {}
+        result = {}
+        group = {}
+        for g0, n in GROUPS:
+            for u in range(n):
+                group[g0 + u] = (g0, n)
         hc = {}
         hs = {}
 
@@ -70,8 +73,7 @@ def tile_list_tabmlp_tm_none_kernel(tc, tab, w1, w2_words, w2_scales, offs, out)
         def gather_words(a, i0, i1, into):
             for i in range(i0, i1):
                 words[a, i] = into[:, JT * (i - i0) : JT * (i - i0 + 1)]
-            offsets = lst[:, JT // 16 * i0 : JT // 16 * i1]
-            nc.vector.tensor_copy(into, table[a][:].bitcast(U32).indirect(offsets))
+            nc.vector.tensor_copy(into, table[a][:].bitcast(U32).indirect(lst[:, JT // 16 * i0 : JT // 16 * i1]))
 
         with tc.tile_pool(name="rows", bufs=1) as rows:
             planes = rows.tile([P, T], U8, name="planes", align_bytes=64)
@@ -117,27 +119,37 @@ def tile_list_tabmlp_tm_none_kernel(tc, tab, w1, w2_words, w2_scales, offs, out)
                 in_=grouped[a][:, 4 * P * t0 : 4 * P * t1],
             )
 
-        def product1(i, a, t0=0, t1=QUARTERS):
-            if a == 0:
-                bank = i if i < BANKS else RING + i % RING
-                acc[i] = psum.tile([P, QUARTERS, JT], F32, name="bank%d" % bank)
+        def product1(tiles, a, t0=0, t1=QUARTERS):
+            for i in tiles:
+                if a == 0:
+                    bank = i if i < BANKS else RING + i % RING
+                    acc[i] = psum.tile([P, QUARTERS, JT], F32, name="bank%d" % bank)
             for t in range(t0, t1):
-                nc.tensor.matmul_mx(
-                    out=acc[i][:, t, :],
-                    lhsT=codes[a, t].bitcast(E4M3),
-                    lhsT_scale=w1s[:, H * a + P * t : H * a + P * t + P],
-                    rhs=words[a, i].bitcast(E4M3),
-                    rhs_scale=gsc[4 * a : P, JT * i : JT * i + JT],
-                    start=(a == 0 and t == 0),
-                    stop=(a == LAST and t == QUARTERS - 1),
-                )
+                for i in tiles:
+                    nc.tensor.matmul_mx(
+                        out=acc[i][:, t, :],
+                        lhsT=codes[a, t].bitcast(E4M3),
+                        lhsT_scale=w1s[:, H * a + P * t : H * a + P * t + P],
+                        rhs=words[a, i].bitcast(E4M3),
+                        rhs_scale=gsc[4 * a : P, JT * i : JT * i + JT],
+                        start=(a == 0 and t == 0),
+                        stop=(a == LAST and t == QUARTERS - 1),
+                    )
+
+        def hold(i):
+            return 4
 
         def relu(i):
-            name = "hc%d" % (i - RING) if i >= RING else "hidden%d" % i
-            hidden[i] = keep.tile([P, QUARTERS * JT], BF16, name=name, align_bytes=64)
-            dst = hidden[i][:].rearrange("p (j t) -> p j t", t=QUARTERS)
-            src = acc[i][:].rearrange("p t j -> p j t")
-            if i == VECTOR_RELU:
+            g0, n = group[i]
+            if i == g0:
+                name = "hc%d" % (i - hold(i)) if i >= RING else "hidden%d" % i
+                whole = keep.tile([P, n * QUARTERS * JT], BF16, name=name, align_bytes=64)
+                for u in range(n):
+                    hidden[g0 + u] = whole[:, QUARTERS * JT * u : QUARTERS * JT * (u + 1)]
+                joined[g0] = whole
+            dst = joined[g0][:].rearrange("p (u x m t) -> p u x m t", u=n, x=n, t=QUARTERS)[:, :, i - g0, :, :]
+            src = acc[i][:].rearrange("p t (m u) -> p u m t", u=n)
+            if i in VECTOR_RELUS:
                 nc.vector.tensor_scalar_max(dst, src, 0.0)
             else:
                 nc.scalar.activation(dst, src, RELU)
@@ -145,19 +157,22 @@ def tile_list_tabmlp_tm_none_kernel(tc, tab, w1, w2_words, w2_scales, offs, out)
         def quantize_h(i):
             hc[i] = keep.tile([P, JT], U32, name="hc%d" % i, align_bytes=64)
             hs[i] = keep.tile([P, JT], U8, name="hs%d" % i, align_bytes=64)
-            nc.vector.quantize_mx(out=hc[i][:].bitcast(E4M3), scales=hs[i][:], in_=hidden[i][:])
+            nc.vector.quantize_mx(out=hc[i][:].bitcast(E4M3), scales=hs[i][:], in_=hidden[i])
 
         def product2(i):
-            ot = ring.tile([P, M], F32, name="ot", align_bytes=64)
-            banks = [2 * i % RING, (2 * i + 1) % RING]
+            g0, size = group[i]
+            if i == g0:
+                result[g0] = keep.tile([P, size * M], F32, name="ot%d" % i, align_bytes=64)
+            ot = result[g0][:, M * (i - g0) : M * (i - g0 + 1)]
+            banks = [(2 * i + 0) % RING, (2 * i + 1 + 0) % RING]
             if i == TILES - 1:
                 banks.extend([RING, RING + 1])
             width = M // len(banks)
-            scalar_turn = 1 if i == TILES - 2 else 0
+            pieces = [(width * n, width * (n + 1), bank, 3 < i < 14 or n % 2 == (i == 14)) for n, bank in enumerate(banks)]
+            pieces = {}.get(i, pieces)
             stored = HALF if i == 0 else M
-            for n, bank in enumerate(banks):
-                c0, c1 = width * n, width * (n + 1)
-                res = psum.tile([P, width], F32, name="bank%d" % bank)
+            for c0, c1, bank, on_scalar in pieces:
+                res = psum.tile([P, c1 - c0], F32, name="bank%d" % bank)
                 nc.tensor.matmul_mx(
                     out=res[:],
                     lhsT=hc[i][:].bitcast(E4M3),
@@ -167,63 +182,74 @@ def tile_list_tabmlp_tm_none_kernel(tc, tab, w1, w2_words, w2_scales, offs, out)
                     start=True,
                     stop=True,
                 )
-                if n % 2 == scalar_turn:
+                if on_scalar:
                     nc.scalar.copy(out=ot[:, c0:c1], in_=res[:])
                 else:
                     nc.vector.tensor_copy(ot[:, c0:c1], res[:])
-                if c1 % stored == 0:
+                if size > 1:
+                    if c1 == M and i == g0 + size - 1:
+                        rows = out[JT * g0 : JT * (g0 + size), :].rearrange("(p u) c -> p (u c)", u=size)
+                        nc.sync.dma_start(rows, result[g0][:])
+                elif c1 % stored == 0:
                     nc.sync.dma_start(out[JT * i : JT * i + JT, c1 - stored : c1], ot[:, c1 - stored : c1])
 
+        early = range(BANKS)
         round_w1(0)
         quantize_w1(0, 0, QUARTERS, w1c[0])
-        for i in range(BANKS):
-            product1(i, 0)
+        product1(early, 0)
         round_w1(1)
         quantize_w1(1, 0, 2, w1c[1])
         gather_words(1, 0, BANKS, second[:, 0 : BANKS * JT])
         gather_words(1, BANKS, GATHERED_EARLY, second[:, BANKS * JT : GATHERED_EARLY * JT])
-        for i in range(BANKS):
-            product1(i, 1, 0, 2)
+        product1(early, 1, 0, 2)
         round_w1(LAST)
         quantize_w1(1, 2, QUARTERS, keep.tile([P, H // 2], U32, name="raw%d" % LAST, align_bytes=64))
-        for i in range(BANKS):
-            product1(i, 1, 2, QUARTERS)
+        product1(early, 1, 2, QUARTERS)
         quantize_w1(LAST, 0, QUARTERS, w1c[LAST])
 
         for i in range(0, FRONT, PAIR):
             gather_words(LAST, i, i + PAIR, front[:, JT * i : JT * (i + PAIR)])
-        for i in range(RING):
-            product1(i, LAST)
+        product1([0], LAST)
+        product1([1], LAST)
+        product1([2], LAST)
+        product1([3], LAST)
         for i in range(RING):
             relu(i)
             if i < 2:
                 quantize_h(i)
-        for i in range(RING, FRONT):
-            product1(i, LAST)
+        product1([4], LAST)
+        product1([5], LAST)
 
-        left = [(i, a) for i in range(BANKS, BANKS + PAIR) for a in range(LAST)]
-        left.extend((i, LAST) for i in range(FRONT, BANKS + PAIR))
-        left.extend((i, a) for i in range(BANKS + PAIR, TILES) for a in range(PASSES))
-        passes = {i: left[PER_STEP * (i - 1) : PER_STEP * i] for i in range(1, TILES)}
+        left = [([i], a) for i in range(BANKS, BANKS + PAIR) for a in range(LAST)]
+        left.extend(([i], LAST) for i in range(FRONT, BANKS + PAIR))
+        left.extend(([i], a) for i in range(BANKS + PAIR, TILES) for a in range(PASSES))
+        steps = [1 + n // 2 for n in range(26)]
+        passes = {}
+        for i, unit in zip(steps, left):
+            passes.setdefault(i, []).append(unit)
         gathers = {}
         for i in range(1, TILES):
-            for u, a in passes[i]:
-                if (a, u) not in words and u % PAIR == 0:
-                    gathers[i - LEAD] = (a, u)
+            for tiles, a in passes.get(i, ()):
+                if (a, tiles[0]) not in words and tiles[0] % PAIR == 0:
+                    gathers.setdefault(max(i - LEAD, 0), []).append((a, tiles[0]))
 
         summed = list(range(RING, FRONT))
+
+        def relu_ready(i):
+            for u in list(summed):
+                if u <= i + hold(u):
+                    relu(u)
+                    summed.remove(u)
+
         for i in range(TILES):
             product2(i)
             if 0 < i < TILES - 1:
                 quantize_h(i + 1)
-            if i in gathers:
-                a, u = gathers[i]
-                gather_words(a, u, u + PAIR, keep.tile([P, PAIR * JT], U32, name="hs%d" % i, align_bytes=64)[:])
-            for u, a in passes.get(i, ()):
-                product1(u, a)
+            for n, (a, u) in enumerate(gathers.get(i, ())):
+                gather_words(a, u, u + PAIR, keep.tile([P, PAIR * JT], U32, name="hs%d" % (i - n), align_bytes=64)[:])
+            relu_ready(i)
+            for tiles, a in passes.get(i, ()):
+                product1(tiles, a)
                 if a == LAST:
-                    summed.append(u)
-            for u in list(summed):
-                if u <= i + RING:
-                    relu(u)
-                    summed.remove(u)
+                    summed.extend(tiles)
+            relu_ready(i)

@@ -40,13 +40,13 @@ def tile_list_tabmlp_tm_none_kernel(tc, tab, w1, w2_words, w2_scales, offs, out)
         keep = ctx.enter_context(tc.tile_pool(name="keep", bufs=1))
         psum = ctx.enter_context(tc.psum_pool(name="psum", bufs=1))
 
-        lst = keep.tile([P, S // 16], U16, name="lst")
+        lst = keep.tile([P, S // 16], U16, name="lst", align_bytes=256)
         nc.sync.dma_start(lst[:], offs)
 
-        table = [keep.tile([P, T], I32, name="table%d" % a, align_bytes=64) for a in range(PASSES)]
-        raw = [keep.tile([P, 4, H], F32, name="raw%d" % a, align_bytes=64) for a in range(PASSES)]
-        w2c = keep.tile([P, 2 * M], U8, name="w2c", align_bytes=64)
-        w2s = keep.tile([P, M], U8, name="w2s", align_bytes=64)
+        table = [keep.tile([P, T], I32, name="table%d" % a, align_bytes=256) for a in range(PASSES)]
+        raw = [keep.tile([P, 4, H], F32, name="raw%d" % a, align_bytes=256) for a in range(PASSES)]
+        w2c = keep.tile([P, 2 * M], U8, name="w2c", align_bytes=256)
+        w2s = keep.tile([P, M], U8, name="w2s", align_bytes=256)
         gsc = keep.tile([P, S], U8, name="gsc", align_bytes=64)
         w1c = [keep.tile([P, H], U32, name="w1c%d" % a, align_bytes=64) for a in range(PASSES)]
         first = keep.tile([P, S], U32, name="first", align_bytes=64)
@@ -76,7 +76,7 @@ def tile_list_tabmlp_tm_none_kernel(tc, tab, w1, w2_words, w2_scales, offs, out)
             nc.vector.tensor_copy(into, table[a][:].bitcast(U32).indirect(lst[:, JT // 16 * i0 : JT // 16 * i1]))
 
         with tc.tile_pool(name="rows", bufs=1) as rows:
-            planes = rows.tile([P, T], U8, name="planes", align_bytes=64)
+            planes = rows.tile([P, T], U8, name="planes", align_bytes=256)
             nc.vector.memset(planes[:].bitcast(I32), 0)
             nc.vector.memset(w2s[:].bitcast(I32), 0)
             load_table(0)
@@ -162,7 +162,7 @@ def tile_list_tabmlp_tm_none_kernel(tc, tab, w1, w2_words, w2_scales, offs, out)
         def product2(i):
             g0, size = group[i]
             if i == g0:
-                result[g0] = keep.tile([P, size * M], F32, name="ot%d" % i, align_bytes=64)
+                result[g0] = keep.tile([P, size * M], F32, name="ot%d" % i, align_bytes=256)
             ot = result[g0][:, M * (i - g0) : M * (i - g0 + 1)]
             banks = [(2 * i + 0) % RING, (2 * i + 1 + 0) % RING]
             if i == TILES - 1:
@@ -203,7 +203,7 @@ def tile_list_tabmlp_tm_none_kernel(tc, tab, w1, w2_words, w2_scales, offs, out)
         gather_words(1, BANKS, GATHERED_EARLY, second[:, BANKS * JT : GATHERED_EARLY * JT])
         product1(early, 1, 0, 2)
         round_w1(LAST)
-        quantize_w1(1, 2, QUARTERS, keep.tile([P, H // 2], U32, name="raw%d" % LAST, align_bytes=64))
+        quantize_w1(1, 2, QUARTERS, keep.tile([P, H // 2], U32, name="raw%d" % LAST, align_bytes=256))
         product1(early, 1, 2, QUARTERS)
         quantize_w1(LAST, 0, QUARTERS, w1c[LAST])
 

@@ -168,9 +168,9 @@ def tile_list_tabmlp_tm_none_kernel(tc, tab, w1, w2_words, w2_scales, offs, out)
             if i == TILES - 1:
                 banks.extend([RING, RING + 1])
             width = M // len(banks)
-            pieces = [(width * n, width * (n + 1), bank, 3 < i < 14 or n % 2 == (i == 14)) for n, bank in enumerate(banks)]
+            pieces = [(width * n, width * (n + 1), bank, 3 < i < 13 or n % 2 == (i == 14)) for n, bank in enumerate(banks)]
             pieces = {}.get(i, pieces)
-            stored = HALF if i == 0 else M
+            stored = HALF if i in (0, TILES - 1) else M
             for c0, c1, bank, on_scalar in pieces:
                 res = psum.tile([P, c1 - c0], F32, name="bank%d" % bank)
                 nc.tensor.matmul_mx(
@@ -239,12 +239,14 @@ def tile_list_tabmlp_tm_none_kernel(tc, tab, w1, w2_words, w2_scales, offs, out)
             for u in list(summed):
                 if u <= i + hold(u):
                     relu(u)
+                    quantize_h(u)
                     summed.remove(u)
 
         for i in range(TILES):
             product2(i)
-            if 0 < i < TILES - 1:
-                quantize_h(i + 1)
+            if i == 0:
+                quantize_h(2)
+                quantize_h(3)
             for n, (a, u) in enumerate(gathers.get(i, ())):
                 gather_words(a, u, u + PAIR, keep.tile([P, PAIR * JT], U32, name="hs%d" % (i - n), align_bytes=64)[:])
             relu_ready(i)

@@ -37,14 +37,15 @@ GROUPS = [(0, 1), (1, 1), (2, 1), (3, 1), (4, 1), (5, 1), (6, 1), (7, 1), (8, 1)
 def tile_list_tabmlp_tm_none_kernel(tc, tab, w1, w2_words, w2_scales, offs, out):
     nc = tc.nc
     with ExitStack() as ctx:
+        big = ctx.enter_context(tc.tile_pool(name="big", bufs=1))
         keep = ctx.enter_context(tc.tile_pool(name="keep", bufs=1))
         psum = ctx.enter_context(tc.psum_pool(name="psum", bufs=1))
 
         lst = keep.tile([P, S // 16], U16, name="lst", align_bytes=256)
         nc.sync.dma_start(lst[:], offs)
 
-        table = [keep.tile([P, T], I32, name="table%d" % a, align_bytes=256) for a in range(PASSES)]
-        raw = [keep.tile([P, 4, H], F32, name="raw%d" % a, align_bytes=256) for a in range(PASSES)]
+        table = [big.tile([P, T], I32, name="table%d" % a, align_bytes=4096, offset=4 * T * a) for a in range(PASSES)]
+        raw = [big.tile([P, 4, H], F32, name="raw%d" % a, align_bytes=4096, offset=4 * T * PASSES + 16 * H * a) for a in range(PASSES)]
         w2c = keep.tile([P, 2 * M], U8, name="w2c", align_bytes=256)
         w2s = keep.tile([P, M], U8, name="w2s", align_bytes=256)
         gsc = keep.tile([P, S], U8, name="gsc", align_bytes=64)
@@ -76,7 +77,7 @@ def tile_list_tabmlp_tm_none_kernel(tc, tab, w1, w2_words, w2_scales, offs, out)
             nc.vector.tensor_copy(into, table[a][:].bitcast(U32).indirect(lst[:, JT // 16 * i0 : JT // 16 * i1]))
 
         with tc.tile_pool(name="rows", bufs=1) as rows:
-            planes = rows.tile([P, T], U8, name="planes", align_bytes=256)
+            planes = rows.tile([P, T], U8, name="planes", align_bytes=4096)
             nc.vector.memset(planes[:].bitcast(I32), 0)
             nc.vector.memset(w2s[:].bitcast(I32), 0)
             load_table(0)
@@ -162,7 +163,7 @@ def tile_list_tabmlp_tm_none_kernel(tc, tab, w1, w2_words, w2_scales, offs, out)
         def product2(i):
             g0, size = group[i]
             if i == g0:
-                result[g0] = keep.tile([P, size * M], F32, name="ot%d" % i, align_bytes=256)
+                result[g0] = big.tile([P, size * M], F32, name="ot%d" % i, align_bytes=4096, offset=(4 * T + 16 * H) * PASSES + 4 * M * i)
             ot = result[g0][:, M * (i - g0) : M * (i - g0 + 1)]
             banks = [(2 * i + 0) % RING, (2 * i + 1 + 0) % RING]
             if i == TILES - 1:
@@ -170,7 +171,7 @@ def tile_list_tabmlp_tm_none_kernel(tc, tab, w1, w2_words, w2_scales, offs, out)
             width = M // len(banks)
             pieces = [(width * n, width * (n + 1), bank, 3 < i < 13 or n % 2 == (i == 14)) for n, bank in enumerate(banks)]
             pieces = {}.get(i, pieces)
-            stored = HALF if i in (0, TILES - 1) else M
+            stored = HALF if i == 0 else M
             for c0, c1, bank, on_scalar in pieces:
                 res = psum.tile([P, c1 - c0], F32, name="bank%d" % bank)
                 nc.tensor.matmul_mx(
@@ -203,7 +204,7 @@ def tile_list_tabmlp_tm_none_kernel(tc, tab, w1, w2_words, w2_scales, offs, out)
         gather_words(1, BANKS, GATHERED_EARLY, second[:, BANKS * JT : GATHERED_EARLY * JT])
         product1(early, 1, 0, 2)
         round_w1(LAST)
-        quantize_w1(1, 2, QUARTERS, keep.tile([P, H // 2], U32, name="raw%d" % LAST, align_bytes=256))
+        quantize_w1(1, 2, QUARTERS, big.tile([P, H // 2], U32, name="held", align_bytes=4096, offset=4 * T * PASSES + 16 * H * LAST))
         product1(early, 1, 2, QUARTERS)
         quantize_w1(LAST, 0, QUARTERS, w1c[LAST])
 

from contextlib import ExitStack

import concourse.mybir as mybir

K, H, M, T, S = 1536, 512, 1024, 4096, 2048
FLOPS = 2 * S * (K * H + H * M)

F32 = mybir.dt.float32
BF16 = mybir.dt.bfloat16
I32 = mybir.dt.int32
U32 = mybir.dt.uint32
U16 = mybir.dt.uint16
U8 = mybir.dt.uint8
E4M3 = mybir.dt.float8_e4m3fn_x4
E2M1 = mybir.dt.float4_e2m1fn_x4
RELU = mybir.ActivationFunctionType.Relu
COPY = mybir.ActivationFunctionType.Copy

P = 128
PASSES = K // 512
LAST = PASSES - 1
QUARTERS = 4
JT = 128
TILES = S // JT
HALF = M // 2
BANKS = 8
RING = 4
PAIR = 2
SCALE_LOADS_ON_SYNC = 1
GATHERED_EARLY = 14
FRONT = 6
LEAD = 2
VECTOR_RELUS = (3,7,8,9,10,11,12,13,14)
GROUPS = [(0, 1), (1, 1), (2, 1), (3, 1), (4, 1), (5, 1), (6, 1), (7, 1), (8, 1), (9, 1), (10, 1), (11, 1), (12, 1), (13, 1), (14, 1), (15, 1)]


def tile_list_tabmlp_tm_none_kernel(tc, tab, w1, w2_words, w2_scales, offs, out):
    nc = tc.nc
    with ExitStack() as ctx:
        big = ctx.enter_context(tc.tile_pool(name="big", bufs=1))
        keep = ctx.enter_context(tc.tile_pool(name="keep", bufs=1))
        psum = ctx.enter_context(tc.psum_pool(name="psum", bufs=1))

        lst = keep.tile([P, S // 16], U16, name="lst", align_bytes=256)
        nc.sync.dma_start(lst[:], offs)

        table = [big.tile([P, T], I32, name="table%d" % a, align_bytes=4096, offset=4 * T * a) for a in range(PASSES)]
        raw = [big.tile([P, 4, H], F32, name="raw%d" % a, align_bytes=4096, offset=4 * T * PASSES + 16 * H * a) for a in range(PASSES)]
        w2c = keep.tile([P, 2 * M], U8, name="w2c", align_bytes=256)
        w2s = keep.tile([P, M], U8, name="w2s", align_bytes=256)
        gsc = keep.tile([P, S], U8, name="gsc", align_bytes=64)
        w1c = [keep.tile([P, H], U32, name="w1c%d" % a, align_bytes=64) for a in range(PASSES)]
        first = keep.tile([P, S], U32, name="first", align_bytes=64)
        words = {}
        grouped = {}
        codes = {}
        acc = {}
        hidden = {}
        joined = {}
        result = {}
        group = {}
        for g0, n in GROUPS:
            for u in range(n):
                group[g0 + u] = (g0, n)
        hc = {}
        hs = {}

        def load_table(a):
            nc.sync.dma_start(table[a][:], tab[a, 0 : 512 * T].rearrange("(p w) -> p w", p=P).bitcast(I32))

        def load_w1(a):
            nc.sync.dma_start(raw[a][:], w1[512 * a : 512 * a + 512, :].rearrange("(p j) c -> p j c", j=4))

        def gather_words(a, i0, i1, into):
            for i in range(i0, i1):
                words[a, i] = into[:, JT * (i - i0) : JT * (i - i0 + 1)]
            nc.vector.tensor_copy(into, table[a][:].bitcast(U32).indirect(lst[:, JT // 16 * i0 : JT // 16 * i1]))

        with tc.tile_pool(name="rows", bufs=1) as rows:
            planes = rows.tile([P, T], U8, name="planes", align_bytes=4096)
            nc.vector.memset(planes[:].bitcast(I32), 0)
            nc.vector.memset(w2s[:].bitcast(I32), 0)
            load_table(0)
            load_w1(0)
            for q in range(4):
                queue = nc.sync if q < SCALE_LOADS_ON_SYNC else nc.gpsimd
                queue.dma_start(
                    planes[32 * q : 32 * q + 4 * PASSES, :].bitcast(I32),
                    tab[:, 512 * T + 4 * T * q : 512 * T + 4 * T * (q + 1)].rearrange("a (r t) -> a r t", r=4).bitcast(I32),
                )
            load_w1(1)
            load_table(1)
            load_w1(LAST)
            load_table(LAST)
            nc.sync.dma_start(w2c[:].bitcast(I32), w2_words[0].bitcast(I32))
            for q in range(4):
                nc.sync.dma_start(w2s[32 * q : 32 * q + 4, :].bitcast(I32), w2_scales[0, 4 * q : 4 * q + 4, :].bitcast(I32))
            gather_words(0, 0, TILES, first[:])
            nc.vector.tensor_copy(gsc[:], planes[:].indirect(lst[:]))

        later = ctx.enter_context(tc.tile_pool(name="later", bufs=1))
        w1s = later.tile([P, PASSES * H], U8, name="w1s", align_bytes=64)
        second = later.tile([P, GATHERED_EARLY * JT], U32, name="second", align_bytes=64)
        front = later.tile([P, FRONT * JT], U32, name="front", align_bytes=64)

        def round_w1(a):
            grouped[a] = keep.tile([P, 4 * H], BF16, name="grouped%d" % a, align_bytes=64)
            nc.scalar.activation(
                grouped[a][:].rearrange("p (t m j) -> p m t j", t=QUARTERS, j=4),
                raw[a][:].rearrange("p j (m t) -> p m t j", t=QUARTERS),
                COPY,
            )

        def quantize_w1(a, t0, t1, into):
            for t in range(t0, t1):
                codes[a, t] = into[:, P * (t - t0) : P * (t - t0 + 1)]
            nc.vector.quantize_mx(
                out=into[:, 0 : P * (t1 - t0)].bitcast(E4M3),
                scales=w1s[:, H * a + P * t0 : H * a + P * t1],
                in_=grouped[a][:, 4 * P * t0 : 4 * P * t1],
            )

        def product1(tiles, a, t0=0, t1=QUARTERS):
            for i in tiles:
                if a == 0:
                    bank = i if i < BANKS else RING + i % RING
                    acc[i] = psum.tile([P, QUARTERS, JT], F32, name="bank%d" % bank)
            for t in range(t0, t1):
                for i in tiles:
                    nc.tensor.matmul_mx(
                        out=acc[i][:, t, :],
                        lhsT=codes[a, t].bitcast(E4M3),
                        lhsT_scale=w1s[:, H * a + P * t : H * a + P * t + P],
                        rhs=words[a, i].bitcast(E4M3),
                        rhs_scale=gsc[4 * a : P, JT * i : JT * i + JT],
                        start=(a == 0 and t == 0),
                        stop=(a == LAST and t == QUARTERS - 1),
                    )

        def hold(i):
            return 4

        def relu(i):
            g0, n = group[i]
            if i == g0:
                name = "hc%d" % (i - hold(i)) if i >= RING else "hidden%d" % i
                whole = keep.tile([P, n * QUARTERS * JT], BF16, name=name, align_bytes=64)
                for u in range(n):
                    hidden[g0 + u] = whole[:, QUARTERS * JT * u : QUARTERS * JT * (u + 1)]
                joined[g0] = whole
            dst = joined[g0][:].rearrange("p (u x m t) -> p u x m t", u=n, x=n, t=QUARTERS)[:, :, i - g0, :, :]
            src = acc[i][:].rearrange("p t (m u) -> p u m t", u=n)
            if i in VECTOR_RELUS:
                nc.vector.tensor_scalar_max(dst, src, 0.0)
            else:
                nc.scalar.activation(dst, src, RELU)

        def quantize_h(i):
            hc[i] = keep.tile([P, JT], U32, name="hc%d" % i, align_bytes=64)
            hs[i] = keep.tile([P, JT], U8, name="hs%d" % i, align_bytes=64)
            nc.vector.quantize_mx(out=hc[i][:].bitcast(E4M3), scales=hs[i][:], in_=hidden[i])

        def product2(i):
            g0, size = group[i]
            if i == g0:
                result[g0] = big.tile([P, size * M], F32, name="ot%d" % i, align_bytes=4096, offset=(4 * T + 16 * H) * PASSES + 4 * M * i)
            ot = result[g0][:, M * (i - g0) : M * (i - g0 + 1)]
            banks = [(2 * i + 0) % RING, (2 * i + 1 + 0) % RING]
            if i == TILES - 1:
                banks.extend([RING, RING + 1])
            width = M // len(banks)
            pieces = [(width * n, width * (n + 1), bank, 3 < i < 13 or n % 2 == (i == 14)) for n, bank in enumerate(banks)]
            pieces = {}.get(i, pieces)
            stored = HALF if i == 0 else M
            for c0, c1, bank, on_scalar in pieces:
                res = psum.tile([P, c1 - c0], F32, name="bank%d" % bank)
                nc.tensor.matmul_mx(
                    out=res[:],
                    lhsT=hc[i][:].bitcast(E4M3),
                    lhsT_scale=hs[i][:],
                    rhs=w2c[:, 2 * c0 : 2 * c1].bitcast(E2M1),
                    rhs_scale=w2s[:, c0:c1],
                    start=True,
                    stop=True,
                )
                if on_scalar:
                    nc.scalar.copy(out=ot[:, c0:c1], in_=res[:])
                else:
                    nc.vector.tensor_copy(ot[:, c0:c1], res[:])
                if size > 1:
                    if c1 == M and i == g0 + size - 1:
                        rows = out[JT * g0 : JT * (g0 + size), :].rearrange("(p u) c -> p (u c)", u=size)
                        nc.sync.dma_start(rows, result[g0][:])
                elif c1 % stored == 0:
                    nc.sync.dma_start(out[JT * i : JT * i + JT, c1 - stored : c1], ot[:, c1 - stored : c1])

        early = range(BANKS)
        round_w1(0)
        quantize_w1(0, 0, QUARTERS, w1c[0])
        product1(early, 0)
        round_w1(1)
        quantize_w1(1, 0, 2, w1c[1])
        gather_words(1, 0, BANKS, second[:, 0 : BANKS * JT])
        gather_words(1, BANKS, GATHERED_EARLY, second[:, BANKS * JT : GATHERED_EARLY * JT])
        product1(early, 1, 0, 2)
        round_w1(LAST)
        quantize_w1(1, 2, QUARTERS, big.tile([P, H // 2], U32, name="held", align_bytes=4096, offset=4 * T * PASSES + 16 * H * LAST))
        product1(early, 1, 2, QUARTERS)
        quantize_w1(LAST, 0, QUARTERS, w1c[LAST])

        for i in range(0, FRONT, PAIR):
            gather_words(LAST, i, i + PAIR, front[:, JT * i : JT * (i + PAIR)])
        product1([0], LAST)
        product1([1], LAST)
        product1([2], LAST)
        product1([3], LAST)
        for i in range(RING):
            relu(i)
            if i < 2:
                quantize_h(i)
        product1([4], LAST)
        product1([5], LAST)

        left = [([i], a) for i in range(BANKS, BANKS + PAIR) for a in range(LAST)]
        left.extend(([i], LAST) for i in range(FRONT, BANKS + PAIR))
        left.extend(([i], a) for i in range(BANKS + PAIR, TILES) for a in range(PASSES))
        steps = [1 + n // 2 for n in range(26)]
        passes = {}
        for i, unit in zip(steps, left):
            passes.setdefault(i, []).append(unit)
        gathers = {}
        for i in range(1, TILES):
            for tiles, a in passes.get(i, ()):
                if (a, tiles[0]) not in words and tiles[0] % PAIR == 0:
                    gathers.setdefault(max(i - LEAD, 0), []).append((a, tiles[0]))

        summed = list(range(RING, FRONT))

        def relu_ready(i):
            for u in list(summed):
                if u <= i + hold(u):
                    relu(u)
                    quantize_h(u)
                    summed.remove(u)

        for i in range(TILES):
            product2(i)
            if i == 0:
                quantize_h(2)
                quantize_h(3)
            for n, (a, u) in enumerate(gathers.get(i, ())):
                gather_words(a, u, u + PAIR, keep.tile([P, PAIR * JT], U32, name="hs%d" % (i - n), align_bytes=64)[:])
            relu_ready(i)
            for tiles, a in passes.get(i, ()):
                product1(tiles, a)
                if a == LAST:
                    summed.extend(tiles)
            relu_ready(i)
